import numpy as np, ml_dtypes
CORES = [40,41,42,43,44,45,46,47]
N = 8
import mx_ref
BF = ml_dtypes.bfloat16
def gentries(a):
    return np.ascontiguousarray(a.reshape(8, 16, -1).transpose(0, 2, 1)).reshape(8, -1)
def gtable(e):
    e = np.asarray(e); return np.ascontiguousarray(e.reshape(8, -1, 16).transpose(0, 2, 1)).reshape(128, -1).astype(np.int32)
def gcols(t, e):
    v = np.concatenate([t.reshape(8, 16, -1, 4), np.zeros((8, 16, 1, 4), BF)], axis=2)
    return np.ascontiguousarray(np.stack([v[g][:, e[g]] for g in range(8)])).reshape(128, -1)
def tile(rs):
    return np.stack(rs, axis=2).reshape(128, -1).astype(BF)
def cut(t, i, w=512):
    return t[:, w * i:w * i + w]
def pick(q, e):
    c = np.concatenate([q[0].reshape(128, -1, 4), np.zeros((128, 1, 4), np.uint8)], axis=1); s = np.concatenate([q[1], np.ones((16, 1), np.uint8)], axis=1)
    return (np.ascontiguousarray(c[:, e].reshape(128, -1)), np.ascontiguousarray(s[:, e]))
def join(*qs):
    return (np.concatenate([q[0] for q in qs], axis=1), np.concatenate([q[1] for q in qs], axis=1))
def put(q, e, v):
    c, s = q[0].reshape(128, -1, 4).copy(), q[1].copy(); c[:, e] = v[0].reshape(128, -1, 4); s[:, e] = v[1]
    return (c.reshape(128, -1), s)
def pk(c, s):
    return (np.ascontiguousarray(c), mx_ref.live(s))
def emit(q):
    return q[0], q[1]
def packed(v, rng):
    q = [mx_ref.quantize(np.ascontiguousarray(v[r])) for r in range(N)]
    return np.stack([a for a, b in q]), np.stack([mx_ref.plane(b, rng) for a, b in q])
def values_of_codes():
    e, c = np.zeros((128, 128, 4), np.float32), np.zeros((128, 2, 4), np.uint8)
    e[np.arange(128), np.arange(128), 0] = 1
    c[:127, :, 0] = np.arange(256).reshape(2, 128).T[:127]
    return mx_ref.matmul(mx_ref.quantize(e.reshape(128, 512).astype(BF)), (c.reshape(128, 8), np.full((16, 2), 127, np.uint8))).T.reshape(-1).astype(np.float64)
CODE_VALUE, SCALE_VALUE = values_of_codes(), 2.0 ** (np.arange(256) - 127.0)
def decode(q):
    return (CODE_VALUE[q[0]].reshape(16, 8, -1, 4) * SCALE_VALUE[q[1]][:, None, :, None] + 0.0).reshape(128, -1).astype(np.float32)
def f(rng, *shape):
    return mx_ref.flush((rng.standard_normal(shape, dtype=np.float32) * np.exp2(rng.integers(-2, 3, shape[:-1] + (1,)))).astype(BF))
def wide(rng, *shape, cols=0):
    v = rng.standard_normal(shape, dtype=np.float32) * np.exp2(rng.integers(-12, 13, shape)).astype(np.float32)
    if cols: v *= np.repeat(np.exp2(rng.integers(-cols, cols + 1, shape[:-2] + (1, shape[-1] // 4))) * (rng.random(shape[:-2] + (1, shape[-1] // 4)) > 0.0625), 4, axis=-1).astype(np.float32)
    return mx_ref.flush(v.astype(BF))
C, A, R = 512, 256, 3
STEP = [1, 2, 4]
def partner(r, t):
    return r ^ STEP[t]
def big(v, k):
    v = v.astype(np.float32) * np.float32(k)
    v[np.abs(v) < np.float32(2.0 ** -16)] = 0
    return v.astype(BF)
def common(w, rng):
    c, p = packed(np.stack([w] * N), rng)
    return {"wc": c, "ws": p}
def weights(rng, q=-1):
    w = big(f(rng, 128, 2048), 1).reshape(128, 4, 128, 4)
    if q >= 0:
        w[16 * q:16 * q + 8] = 0
        for i in range(16 * q, 16 * q + 8):
            w[:, :, i] = 0
            for b in range(4): w[i, b, i, b] = 64
    return common(w.reshape(128, 2048), rng)
def numbers_of(rng):
    return {"x": big(f(rng, N, 128, 4 * C), 1), "u": np.array(f(rng, N, 128, 512)), "v": np.array(f(rng, N, 128, 512))}
def lists_of(rng):
    return {"m": np.argsort(rng.random((N, 8, C)), axis=2), "la": rng.integers(0, C, (N, 8, R * A)), "lb": rng.integers(0, C, (N, 8, R * A)),
            "ld": np.argsort(rng.random((N, 8, R, C)), axis=3)[:, :, :, :A].reshape(N, 8, R * A)}
def stored(l):
    return {k: np.stack([gtable(e) for e in l[k]]) for k in ("m", "la", "lb", "ld")}
def setup_inputs(rng):
    return {**numbers_of(rng), **stored(lists_of(rng)), **weights(rng)}
def setup_inputs_rolls(rng):
    d, l = numbers_of(rng), lists_of(rng)
    q = int(rng.integers(8))
    o = rng.permutation(N)
    back = []
    for r in range(N):
        g = rng.permutation(8)
        if o[r] % 3 == 2: g = rng.permutation(7)
        while abs(int(g[0]) - int(g[1])) < 2: g = np.roll(g, 1)
        back.append([[(0, 1), (1, 2), (2, 3)], [(0, 1), (2, 3), (0, 2)], [(0, 1), (0, 1), (0, 1)]][o[r] % 3])
        back[r] = [[int(g[i]) for i in e] for e in back[r]]
    size = np.exp2(np.array([-30.0, -12.0, 0.0, 10.0])[rng.permutation(N) % 4]).astype(np.float32)
    mark = np.zeros((27, 8, 4), np.float32)
    for k in range(9):
        for i in range(2):
            mark[k + 9 * i, :, 0] = i
            if k < 8: mark[k + 9 * i, k] = (0, 2, 0, 0)
        mark[18 + k, :, 1] = 2
        if k < 8: mark[18 + k, k] = 0
    x = d["x"].reshape(N, 8, 16, C, 4)
    u = d["u"].reshape(N, 128, 128, 4)
    u[:, :, ::16] = 0
    one = np.ones(N, np.float32)
    for r in range(N):
        if size[r] < 2.0 ** -20:
            for t in range(R): one[partner(r, t)] = 2.0 ** -30
    for g in range(8):
        u[:, 16 * q + g, 16 * g, 0] = one.astype(BF)
        u[:, 16 * q + g, 16 * g, 1] = (-one).astype(BF)
    for r in range(N):
        e = rng.permutation(C)
        written, pool = e[:A], e[A:]
        kind = rng.integers(0, 27, C)
        kind[l["m"][r, q, pool]] = np.arange(C - A) % 27
        x[r, q, :8] = (mark[kind].transpose(1, 0, 2) * size[r]).astype(BF)
        for t in range(R):
            l["ld"][r, q, A * t:A * t + A] = rng.permutation(written)
            p = back[partner(r, t)][t]
            most = o[partner(r, t)] == 2 and t == R - 1
            h = A - 1 if most else int(rng.integers(2, A // 4))
            n = np.full(8, h - 1)
            if (o[partner(r, t)] + t) % 2 == 0:
                n[min(p):] = h
                n[max(p)] = h + 1
            else:
                n[p] = h
                n[max(p) + 1:] = h
            k = np.full(2 * A, 8)
            if most: k[:A] = 26
            s = np.repeat(18 + np.arange(8), A - n) if most else np.repeat(np.arange(8), n)
            k[:len(s)] = s
            e = pool[k + 9 * rng.integers(0, 2, 2 * A) * (k < 9) + 27 * rng.integers(0, (C - A) // 27, 2 * A)]
            j = rng.permutation(A)
            l["la"][r, q, A * t:A * t + A] = e[:A][j]
            l["lb"][r, q, A * t:A * t + A] = e[A:][j]
    return {"x": x.reshape(N, 128, 4 * C), "u": u.reshape(N, 128, 512), "v": d["v"], **stored(l), **weights(rng, q)}
def setup_inputs_lists(rng):
    d, l = numbers_of(rng), lists_of(rng)
    o = rng.permutation(N)
    for r in range(N):
        if o[r] == 2:
            l["m"][r] = rng.permutation(C)[None, :]
            e = l["m"][r, 0, C - 8:]
            x = np.zeros((128, C, 4), BF)
            x[:, e] = d["x"][r].reshape(128, C, 4)[:, e]
            d["x"][r] = x.reshape(128, 4 * C)
            l["la"][r] %= C - 8
            l["lb"][r] %= C - 8
            l["ld"][r] = np.argsort(rng.random((8, R, C - 8)), axis=2)[:, :, :A].reshape(8, R * A)
        elif o[r] % 2:
            e = np.repeat(l["ld"][r, :, :1], R * A, axis=1)
            l["la"][r] = e
            l["lb"][r] = e
        else:
            e = l["ld"][r, :, :A].copy()
            l["ld"][r] = np.tile(e, (1, R))
            l["la"][r] = np.tile(e, (1, R))
            l["lb"][r] = np.tile(e[:, ::-1], (1, R))
    return {**d, **stored(l), **weights(rng)}
def setup_inputs_huge(rng):
    d, l = numbers_of(rng), lists_of(rng)
    o = rng.permutation(N)
    g = np.ones((N, 8))
    for r in range(N):
        if o[r] == 0: g[r] = -1
        if o[r] == 2: g[r, 0] = -1
        if o[r] > 2: g[r] = rng.permutation(8) % 2 * 2.0 - 1.0
    x = 2.0 ** 28 * (1.5 + 0.5 * rng.random((N, 128, 4 * C)))
    u = d["u"].reshape(N, 128, 128, 4)
    u[:, :, ::16] = (2.0 ** 30 * (0.75 + 0.25 * rng.random((N, 128, 8, 4))) * g[:, None, :, None]).astype(np.float32).astype(BF)
    w = np.zeros((128, 4, 128, 4), np.float32)
    i = np.arange(128)
    for b in range(4): w[i, b, i, b] = 32
    return {"x": x.astype(np.float32).astype(BF), "u": u.reshape(N, 128, 512), "v": d["v"], **stored(l), **common(w.reshape(128, 2048).astype(BF), rng)}
def setup_inputs_spread(rng):
    d = setup_inputs(rng)
    d["x"] = big(wide(rng, N, 128, 4 * C, cols=6), 1)
    return d
def check_inputs(d):
    b = []
    for k in ("x", "u", "v"):
        a = np.abs(d[k].astype(np.float32))
        if not (np.isfinite(a).all() and ((a == 0) | (a >= 2.0 ** -30) & (a <= 2.0 ** 30)).all()): b.append("a value of " + k)
    for r in range(N):
        if (np.sort(gentries(d["m"][r]), axis=1) != np.arange(C)).any(): b.append("m: a group's entries aren't a permutation")
        for k in ("la", "lb", "ld"):
            if ((d[k][r] < 0) | (d[k][r] >= C)).any(): b.append("an entry of " + k)
        s = np.sort(gentries(d["ld"][r]).reshape(8, R, A), axis=2)
        if (s[:, :, 1:] == s[:, :, :-1]).any(): b.append("ld: equal entries of a group in a round")
    if (d["wc"] != d["wc"][:1]).any(): b.append("wc differs between ranks")
    s = [mx_ref.live(p) for p in d["ws"]]
    if any((p != s[0]).any() for p in s): b.append("ws differs between ranks")
    return b
def reference(x, u, v, m, la, lb, ld, wc, ws):
    w = pk(wc[0], ws[0])
    qu = [mx_ref.quantize(u[r]) for r in range(N)]
    kept = [x[r] for r in range(N)]
    maps = [[gentries(m[r]).astype(np.int64)] for r in range(N)]
    for t in range(R):
        sent = []
        for r in range(N):
            now = maps[r][t]
            one = gcols(kept[r], np.take_along_axis(now, gentries(la[r])[:, A * t:A * t + A], axis=1))
            two = gcols(kept[r], np.take_along_axis(now, gentries(lb[r])[:, A * t:A * t + A], axis=1))
            q = mx_ref.quantize((one.astype(np.float32) + two.astype(np.float32)).astype(BF))
            h = tile([np.maximum(mx_ref.matmul(pick(w, np.arange(128 * b, 128 * b + 128)), q), np.float32(0.0)) * np.float32(0.015625) for b in range(4)])
            sent.append(mx_ref.quantize(h))
        came = decode(join(*sent)).astype(BF)
        for r in range(N):
            e = partner(r, t)
            yes = mx_ref.matmul(qu[r], sent[e])[::16] + np.float32(0.0) >= 0
            kept[r] = np.concatenate([kept[r], cut(came, e, 4 * A)], axis=1)
            to = gentries(ld[r])[:, A * t:A * t + A]
            new = maps[r][t].copy()
            for g in range(8): new[g, to[g][yes[g]]] = C + A * t + np.flatnonzero(yes[g])
            n = np.sum(~yes, axis=1)
            for g in np.argsort(-n, kind="stable")[:2]: new[g] = maps[r][max(t - 1, 0)][g]
            maps[r].append(new)
    y, om = np.zeros((N, 128, C), np.float32), np.zeros((N, 8, C), np.float32)
    oc, osc = np.zeros((N, 128, 4 * C), np.uint8), np.zeros((N, 16, C), np.uint8)
    for r in range(N):
        q = mx_ref.quantize(gcols(kept[r], maps[r][R]))
        y[r] = mx_ref.matmul(mx_ref.quantize(v[r]), q)
        om[r] = maps[r][R]
        oc[r], osc[r] = emit(q)
    return {"y": y, "om": om, "oc": oc, "osc": osc}

@@ -1,0 +1,692 @@
+import math
+import numpy as np
+from concourse.bass import DstId, RemoteDMATransfer
+from concourse.mybir import dt, AluOpType, AxisListType, ActivationFunctionType
+
+OP = AluOpType
+AF = ActivationFunctionType
+R = 3
+STEP = [1, 2, 4]
+LIFT = 1024
+SL = 1280
+UNIT = 2048.0
+HALF = "float16"
+SPLIT = (0, 3, 5)
+COSTS = [(1.0, 160.0, 1.5, 3.5, 1900.0, 140.0), (1.0, 280.0, 1.3, 3.0, 2200.0, 190.0), (1.2, 120.0, 1.8, 4.5, 1800.0, 170.0),
+         (0.85, 220.0, 1.5, 3.5, 2500.0, 220.0)]
+TRIES, HEAT = 16000, 12.0
+PLAN = {}
+
+SCRATCH = {
+    "Lst": ("sbuf", [128, 176], "int32"),
+    "X0": ("sbuf", [128, 2048], "bfloat16"),
+    "F": ("sbuf", [128, 4 * SL], "bfloat16"),
+    "Ag": ("sbuf", [128, 3072], "bfloat16"),
+    "Z": ("sbuf", [128, 3072], "bfloat16"),
+    "Hb": ("sbuf", [128, 3072], "bfloat16"),
+    "Tt": ("sbuf", [128, 2048], "bfloat16"),
+    "uin": ("sbuf", [128, 512], "bfloat16"),
+    "vin": ("sbuf", [128, 512], "bfloat16"),
+    "ones": ("sbuf", [128, 520], "bfloat16"),
+    "ez": ("sbuf", [128, 520], "bfloat16"),
+    "sw": ("sbuf", [128, 32], "bfloat16"),
+    "st": ("sbuf", [128, 512], "bfloat16"),
+    "idw": ("sbuf", [128, 512], "bfloat16"),
+    "m0r": ("sbuf", [128, 512], "bfloat16"),
+    "jr1": ("sbuf", [128, 256], "bfloat16"),
+    "Dd": ("sbuf", [128, 1536], "bfloat16"),
+    "sgw": ("sbuf", [128, 3 * 272], "bfloat16"),
+    "val": ("sbuf", [128, 272], "bfloat16"),
+    "sg2": ("sbuf", [128, 3 * 256], "bfloat16"),
+    "gx": ("sbuf", [128, 256 * 24], "bfloat16"),
+    "gy": ("sbuf", [128, 256 * 20], HALF),
+    "d1": ("sbuf", [128, 12 * 768 + 64], HALF),
+    "d0": ("sbuf", [128, 6 * 96], "float32"),
+    "rs": ("sbuf", [128, 6 * 96], "float32"),
+    "smi": ("sbuf", [128, 320], "int32"),
+    "smf": ("sbuf", [128, 2560], "float32"),
+    "smu": ("sbuf", [128, 1280], "uint16"),
+    "yo": ("sbuf", [128, 512], "float32"),
+    "ps": ("psum", [128, 4096], "float32"),
+    "wq": ("sbuf", [128, 512], "float8_e4m3fn_x4"), "wqs": ("sbuf", [128, 512], "uint8"),
+    "uq": ("sbuf", [128, 128], "float8_e4m3fn_x4"), "uqs": ("sbuf", [128, 128], "uint8"),
+    "up": ("sbuf", [128, 256], "float8_e4m3fn_x4"), "ups": ("sbuf", [128, 256], "uint8"),
+    "vq": ("sbuf", [128, 128], "float8_e4m3fn_x4"), "vqs": ("sbuf", [128, 128], "uint8"),
+    "eq": ("sbuf", [128, 512], "float8_e4m3fn_x4"), "eqs": ("sbuf", [128, 512], "uint8"),
+    "oq": ("sbuf", [128, 512], "float8_e4m3fn_x4"), "oqs": ("sbuf", [128, 512], "uint8"),
+}
+for _t in range(R):
+    for _n in ("qz", "lz", "qh"):
+        SCRATCH["%s%d" % (_n, _t)] = ("sbuf", [128, 256], "float8_e4m3fn_x4")
+        SCRATCH["%ss%d" % (_n, _t)] = ("sbuf", [128, 256], "uint8")
+ENG = {"v": "ve", "s": "ac", "t": "pe", "g": "gp"}
+LOADS = ["lm", "lx", "ll", "lu", "lw", "lv"]
+STORES = ["so0", "so1", "so2", "so3", "sy0", "sy1", "sy2", "sy3", "som", "sos"]
+SEMAPHORES = ["ve", "ac", "pe", "gp", "sent"] + ["arr%d%d" % (t, h) for t in range(R) for h in range(2)] + LOADS + STORES
+MAIN = ("zl", "Fn", "A", "Z", "qz", "lz", "H", "qh", "flag", "lim", "T", "oq", "yo")
+
+
+def price(o, q, c):
+    fix, cyc, gat, sca = o["q"][q][1]
+    return c[5] if q == "t" else fix + c[0] * (cyc + c[2] * gat + c[3] * sca)
+
+
+def make_plan(ops, ready):
+    n = len(ops)
+    pred, succ, wrote, read = [[] for _ in ops], [[] for _ in ops], {}, {}
+    for i, o in enumerate(ops):
+        p = {}
+        for k in o["w"]:
+            for j in read.get(k, []) + ([wrote[k]] if k in wrote else []):
+                p[j] = False
+        for k in o["r"]:
+            if k in wrote:
+                p[wrote[k]] = True
+        for k in o["r"]:
+            read.setdefault(k, []).append(i)
+        for k in o["w"]:
+            wrote[k], read[k] = i, []
+        p.pop(i, None)
+        pred[i] = sorted(p.items())
+        for j in p:
+            succ[j].append(i)
+    first = [max([ready.get(k, 0.0) for k in o["r"]] + [0.0]) for o in ops]
+    lag = [[c[4] if o["kind"] == "send" else 1700.0 if o["kind"] == "dma" else 0.0 for o in ops] for c in COSTS]
+    cost = [[{q: price(o, q, c) for q in o["q"]} for o in ops] for c in COSTS]
+    busy = [o.get("busy", 0.0) for o in ops]
+    weight = [0.3 / n if o["w"][0][0] in MAIN else 0.0 for o in ops]
+    rank = [0.0] * n
+    for i in range(n - 1, -1, -1):
+        rank[i] = min(cost[0][i].values()) + lag[0][i] + max([COSTS[0][1] + rank[j] for j in succ[i]] + [0.0])
+
+    def greedy():
+        free, fin, start, where, left = {}, [0.0] * n, [0.0] * n, [""] * n, [len(p) for p in pred]
+        cand = [i for i in range(n) if not left[i]]
+        for _ in range(n):
+            best = []
+            for i in cand:
+                opt = []
+                for q in ops[i]["q"]:
+                    t = max(first[i], free.get(q, 0.0))
+                    for j, raw in pred[i]:
+                        t = max(t, fin[j] + COSTS[0][1] if raw or where[j] != q else start[j])
+                    opt.append((t + cost[0][i][q] + (60.0 if q == "v" and len(ops[i]["q"]) > 1 else 0.0), t, q))
+                best.append((min(opt), i))
+            soon = min(b[0][1] for b in best)
+            (_, t, q), i = max((b for b in best if b[0][1] <= soon + 120.0), key=lambda b: (rank[b[1]], -b[1]))
+            start[i], where[i] = t, q
+            free[q] = t + cost[0][i][q]
+            fin[i] = free[q] + lag[0][i]
+            cand.remove(i)
+            for j in succ[i]:
+                left[j] -= 1
+                if not left[j]:
+                    cand.append(j)
+        return sorted(range(n), key=lambda i: (start[i], i)), where
+
+    free, start, fin = [None] * len(COSTS), [None] * len(COSTS), [None] * len(COSTS)
+
+    def span(seq, where, a):
+        total = 0.0
+        for k, c in enumerate(COSTS):
+            wake, ck, lk, snap, sk, fk = c[1], cost[k], lag[k], free[k][:a + 1], start[k], fin[k]
+            f5, end, late = snap[a]
+            f5 = dict(f5)
+            for i in seq[a:]:
+                q = where[i]
+                t = first[i]
+                f = f5[q]
+                if f > t:
+                    t = f
+                for j, raw in pred[i]:
+                    f = fk[j] + wake if raw or where[j] != q else sk[j]
+                    if f > t:
+                        t = f
+                sk[i] = t
+                f = t + ck[i][q]
+                f5[q] = f
+                if busy[i]:
+                    f = max(f + lk[i], f5["e"]) + busy[i]
+                    f5["e"] = f
+                    f += 500.0
+                else:
+                    f += lk[i]
+                fk[i] = f
+                late += f * weight[i]
+                if f > end:
+                    end = f
+                snap.append((dict(f5), end, late))
+            free[k] = snap
+            total += end + late
+        return total
+
+    for k in range(len(COSTS)):
+        free[k], start[k], fin[k] = [({"v": 0.0, "s": 0.0, "t": 0.0, "g": 0.0, "y": 0.0, "e": 0.0}, 0.0, 0.0)], [0.0] * n, [0.0] * n
+    seq, where = greedy()
+    seed = [12345]
+
+    def draw(m):
+        seed[0] = (seed[0] * 1103515245 + 12345) % 2147483648
+        return (seed[0] >> 8) % m
+
+    now = span(seq, where, 0)
+    kept = (now, list(seq), list(where))
+    pos = [0] * n
+    for k, i in enumerate(seq):
+        pos[i] = k
+    both = [i for i in range(n) if len(ops[i]["q"]) > 1]
+    for it in range(TRIES):
+        heat = HEAT * (1.0 - it / TRIES) + 0.1
+        flip = draw(6) == 0
+        i = both[draw(len(both))] if flip else draw(n)
+        a = b = pos[i]
+        if not flip:
+            lo = max([pos[j] for j, _ in pred[i]] + [-1]) + 1
+            hi = min([pos[j] for j in succ[i]] + [n]) - 1
+            if hi <= lo:
+                continue
+            if draw(3):
+                d = 1 if draw(2) else -1
+                b = a + d
+                while lo <= b <= hi and where[seq[b]] != where[i]:
+                    b += d
+            else:
+                b = max(lo, a - 60) + draw(min(hi, a + 60) - max(lo, a - 60) + 1)
+            if b == a or b < lo or b > hi:
+                continue
+        old = (where[i], list(free), [list(s) for s in start], [list(s) for s in fin])
+        if flip:
+            where[i] = [q for q in sorted(ops[i]["q"]) if q != where[i]][0]
+        else:
+            seq.insert(b, seq.pop(a))
+        new = span(seq, where, min(a, b))
+        if new <= now or draw(10000) < 10000 * math.exp((now - new) / heat):
+            now = new
+            for k in range(min(a, b), max(a, b) + 1):
+                pos[seq[k]] = k
+            if now < kept[0]:
+                kept = (now, list(seq), list(where))
+        else:
+            where[i] = old[0]
+            seq.insert(a, seq.pop(b))
+            for k in range(len(COSTS)):
+                free[k], start[k], fin[k] = old[1][k], old[2][k], old[3][k]
+    return [(i, kept[2][i]) for i in kept[1]]
+
+
+def rank_program(g, core, T, topo):
+    rank = T.rank_of(core)
+    if rank is None:
+        return
+    queue = {"v": g.vector, "s": g.scalar, "t": g.tensor, "g": g, "y": g.sync}
+    count = {}
+    known = {q: {} for q in queue}
+    writer, readers = {}, {}
+    ops = []
+
+    def need(q, ev):
+        sem, val, snap = ev
+        k = known[q]
+        if k.get(sem, 0) < val:
+            queue[q].wait_ge(T.sem[sem], val)
+            k[sem] = val
+        for s in snap:
+            if k.get(s, 0) < snap[s]:
+                k[s] = snap[s]
+
+    def gate(q, r, w):
+        own = ENG.get(q)
+        evs = [writer[k] for k in r]
+        for k in w:
+            if k in writer and writer[k][0] != own:
+                evs.append(writer[k])
+            evs += [e for e in readers.get(k, {}).values() if e[0] != own]
+        for e in sorted(evs, key=lambda e: -e[1]):
+            need(q, e)
+
+    def note(ev, r, w):
+        for k in w:
+            writer[k] = ev
+            readers[k] = {}
+        for k in r:
+            readers.setdefault(k, {})[ev[0]] = ev
+
+    def dmas(q, sem, pairs, r=(), w=()):
+        gate(q, r, w)
+        for out, in_ in pairs:
+            queue[q].dma_start(out, in_).then_inc(T.sem[sem], 16)
+            count[sem] = count.get(sem, 0) + 16
+        note((sem, count[sem], dict(known[q])), r, w)
+
+    def emit(o, q):
+        call = o["q"][q][0]
+        if o["kind"] != "call":
+            call(q)
+            return
+        gate(q, o["r"], o["w"])
+        sem = ENG[q]
+        call(queue[q]).then_inc(T.sem[sem], 1)
+        count[sem] = count.get(sem, 0) + 1
+        note((sem, count[sem], dict(known[q])), o["r"], o["w"])
+
+    def op(qs, r, w, kind="call"):
+        ops.append({"q": qs, "r": list(r), "w": list(w), "kind": kind})
+
+    used = {"smf": 0, "smu": 0, "smi": 0, "gx": 0, "gy": 0}
+
+    def small(n, buf="smf"):
+        a = -(-used[buf] // (32 if n > 8 else 8)) * (32 if n > 8 else 8)
+        used[buf] = a + n
+        return T[buf][:, a:a + n], (buf, a), a
+
+    def V(call, n, r=(), w=()):
+        op({"v": (call, (0.0, max(64, n), 0, 0))}, r, w)
+
+    def G(call, n, r=(), w=()):
+        op({"g": (call, (150.0, 2 * n, 0, 0))}, r, w)
+
+    def ts(out, in0, s1, s2, op0, op1, r, w, n=32):
+        if op1 is None:
+            V(lambda e: e.tensor_scalar(out, in0, s1, s2, op0), n, r, w)
+        else:
+            V(lambda e: e.tensor_scalar(out, in0, s1, s2, op0, op1), n, r, w)
+
+    def tt(out, a, b, o, r, w, n=64):
+        V(lambda e: e.tensor_tensor(out, a, b, o), n, r, w)
+
+    def copy(out, in_, n, r, w, gather):
+        c = ((50.0, 0, n, 0), (65.0, 0, n, 0)) if gather else ((0.0, max(64, n), 0, 0), (0.0, max(64, n), 0, 0))
+        op({"v": (lambda e: e.tensor_copy(out, in_), c[0]), "s": (lambda e: e.activation(out, in_, AF.Copy), c[1])}, r, w)
+
+    def affine(out, in_, scale, bias, r, w, n=32):
+        op({"v": (lambda e: e.tensor_scalar(out, in_, scale, bias, OP.mult, OP.add), (0.0, max(64, n), 0, 0)),
+            "s": (lambda e: e.activation(out, in_, AF.Copy, bias=bias, scale=scale), (0.0, max(64, n), 0, 0))}, r, w)
+
+    def fill(out, v, n, cycles, key):
+        op({"v": (lambda e: e.memset(out, float(v)), (0.0, cycles, 0, 0)),
+            "g": (lambda e: e.iota(out, [[0, n]], v, 0, allow_small_or_imprecise_dtypes=True), (150.0, 2 * n, 0, 0))}, [], [key])
+
+    def pick(win, wkeys, off, okey):
+        i = used["gx"]
+        used["gx"] = i + 1
+        out = T.gx[:, 256 * i:256 * i + 256]
+        copy(out, win.indirect(off), 256, list(wkeys) + [okey], [("gx", i)], True)
+        return out, [("gx", i)]
+
+    def scan(rows):
+        first = used["gy"]
+        for row, keys in rows:
+            i = used["gy"]
+            used["gy"] = i + 1
+            V(lambda e, i=i, row=row: e.tensor_tensor_scan(T.gy[:, 256 * i:256 * i + 256], T.st[:, 0:256], row, 0.0, OP.add, OP.max),
+              128, keys + [("st", 0)], [("gy", i)])
+        return T.gy[:, 256 * first + 15:256 * first + 256 * len(rows):16], [("gy", first + k) for k in range(len(rows))]
+
+    L = T.Lst
+    dmas("y", "lm", [(L[:, 0:32], T.m[:])], w=["m_"])
+    dmas("s", "lm", [(L[:, 80:128], T.lb[:])], w=["lb_"])
+    dmas("y", "lm", [(L[:, 32:80], T.la[:])], w=["lists"])
+    writer["lists"] = ("lm", 48, {})
+    dmas("s", "ll", [(L[:, 128:176], T.ld[:])], w=["ld_"])
+    dmas("y", "lx", [(T.X0[:], T.x[:])], w=["X0"])
+    dmas("y", "lu", [(T.uin[:], T.u[:])], w=["uin"])
+    dmas("y", "lw", [(T.wq[:].bitcast(dt.uint8), T.wc[:]), (T.wqs[:], T.ws[:])], w=["wq"])
+    dmas("y", "lv", [(T.vin[:], T.v[:])], w=["vin"])
+    ready = {"lists": 2300.0, "ld_": 2350.0, "X0": 4600.0, "uin": 5200.0, "wq": 6800.0, "vin": 7300.0}
+
+    vI, kvI, _ = small(32, "smi")
+    pI, kpI, _ = small(32, "smi")
+    kI, kkI, akI = small(32, "smi")
+    G(lambda e: e.iota(vI, [[-1, 32]], 512, 1), 32, w=[kvI])
+    G(lambda e: e.iota(pI, [[0, 32]], 0, 1), 32, w=[kpI])
+    G(lambda e: e.iota(T.idw[:], [[1, 512]], -256, 0, allow_small_or_imprecise_dtypes=True), 512, w=["idw"])
+    G(lambda e: e.iota(kI, [[16, 32]], 0, 0), 32, w=[kkI])
+    G(lambda e: e.iota(T.jr1[:], [[1, 256]], 1, 0, allow_small_or_imprecise_dtypes=True), 256, w=["jr1"])
+    eps, keps, _ = small(1)
+    zero, kzero, _ = small(32)
+    low, klow, _ = small(96)
+    fill(T.d0[:], -16, 576, 576, "d0")
+    V(lambda e: e.memset(low, -1.0), 96, w=[klow])
+    V(lambda e: e.memset(zero, 0.0), 32, w=[kzero])
+    for t in range(R):
+        fill(T.Dd[:, 512 * t:512 * t + 512], 0, 512, 256, "D%d" % t)
+        V(lambda e, t=t: e.memset(T.sgw[:, 272 * t:272 * t + 1], -1.0), 1, w=[("pad", t)])
+    V(lambda e: e.memset(T.val[:, 0:1], -256.0), 1, w=[("pad", R)])
+    V(lambda e: e.memset(eps, 1e-37), 1, w=[keps])
+    vJ, kvJ, _ = small(32, "smi")
+    p15, kp15, ap15 = small(32, "smi")
+    p7, kp7, ap7 = small(32, "smi")
+    p31, kp31, _ = small(32, "smi")
+    pg, kpg, apg = small(32, "smi")
+    s_a, ks_a, _ = small(32)
+    s_b, ks_b, _ = small(32)
+    r16, kr16, _ = small(16, "smu")
+    ts(vJ, vI, 15, None, OP.bitwise_and, None, [kvI], [kvJ])
+    ts(p15, pI, 15, None, OP.bitwise_and, None, [kpI], [kp15])
+    ts(s_a, vJ, 15, LIFT, OP.is_equal, OP.mult, [kvJ], [ks_a])
+    ts(s_b, vJ, 0, -2 * LIFT, OP.is_equal, OP.mult, [kvJ], [ks_b])
+    V(lambda e: e.tensor_copy(r16, T.smi[:, ap15:ap15 + 16]), 16, [kp15], [kr16])
+    tt(T.sw[:], s_a, s_b, OP.add, [ks_a, ks_b], ["sw"])
+    copy(T.st[:, 0:256], T.sw[:].indirect(r16), 256, ["sw", kr16], [("st", 0)], True)
+    op({"s": (lambda e: e.activation(T.st[:, 256:512], T.sw[:].indirect(r16), AF.Copy, scale=1.0 / LIFT), (65.0, 0, 256, 0))}, ["sw", kr16], [("st", 256)])
+    lift, klift, _ = small(1)
+    last, klast, _ = small(1)
+    ts(lift, T.smi[:, ap15:ap15 + 1], 15, LIFT, OP.is_lt, OP.mult, [kp15], [klift])
+    ts(last, T.smi[:, ap15:ap15 + 1], 15, 2.0, OP.is_equal, OP.subtract, [kp15], [klast])
+    half1, khalf1, _ = small(1)
+    ts(half1, last, 0.5, None, OP.add, None, [klast], [khalf1])
+    mcol, kmcol, _ = small(1)
+    ts(mcol, lift, -1.0, float(256 - SL), OP.mult, OP.add, [klift], [kmcol])
+    down = []
+    for p in range(4):
+        down.append(small(1))
+        ts(down[p][0], lift, -4.0, float(1024 + p), OP.mult, OP.add, [klift], [down[p][1]])
+    mlift, kmlift, _ = small(1)
+    ts(mlift, lift, -1.0, None, OP.mult, None, [klift], [kmlift])
+    slot = []
+    for t in range(R):
+        slot.append(small(1))
+        ts(slot[t][0], lift, -1.0, float(511 + 256 * t - SL), OP.mult, OP.add, [klift], [slot[t][1]])
+    fill(T.ones[:], 1, 520, 260, "ones")
+    G(lambda e: e.affine_select(T.ez[:], T.ones[:], [[-1, 520]], OP.is_equal, 0.0, 4, 4), 520, ["ones"], ["ez"])
+    f_a, kf_a, _ = small(32)
+    f_b, kf_b, _ = small(32)
+    fr8, kfr8, _ = small(32)
+    gfr, kgfr, _ = small(1)
+    U16, kU16, u0 = small(16, "smu")
+    ts(p7, pI, 7, None, OP.bitwise_and, None, [kpI], [kp7])
+    ts(p31, pI, 31, None, OP.bitwise_and, None, [kpI], [kp31])
+    ts(pg, pI, 4, None, OP.arith_shift_right, None, [kpI], [kpg])
+    ts(f_a, p31, 0.125, None, OP.mult, None, [kp31], [kf_a])
+    ts(f_b, p31, 8, -8192.0, OP.is_ge, OP.mult, [kp31], [kf_b])
+    tt(fr8, f_a, f_b, OP.add, [kf_a, kf_b], [kfr8])
+    ts(gfr, T.smi[:, apg:apg + 1], 0.125, None, OP.mult, None, [kpg], [kgfr])
+    V(lambda e: e.tensor_copy(T.smu[:, u0:u0 + 8], T.smi[:, akI:akI + 8]), 8, [kkI], [(kU16, 0)])
+    ts(T.smu[:, u0 + 8:u0 + 16], T.smi[:, ap7:ap7 + 8], 16, None, OP.mult, None, [kp7], [(kU16, 1)])
+
+    L16, kL16, l0 = small(128, "smu")
+    D16, kD16, d0 = small(48, "smu")
+    V(lambda e: e.tensor_copy(T.smu[:, l0:l0 + 32], L[:, 0:32]), 32, ["lists"], [(kL16, 0)])
+    V(lambda e: e.tensor_copy(T.smu[:, l0 + 32:l0 + 128], L[:, 32:128]), 96, ["lists"], [(kL16, 1)])
+
+    def la16(t):
+        return T.smu[:, l0 + 32 + 16 * t:l0 + 48 + 16 * t], (kL16, 1)
+
+    def lb16(t):
+        return T.smu[:, l0 + 80 + 16 * t:l0 + 96 + 16 * t], (kL16, 1)
+
+    def inverse(t):
+        op({"v": (lambda e: e.tensor_copy(T.Dd[:, 512 * t:512 * t + 512].indirect(T.smu[:, d0 + 16 * t:d0 + 16 * t + 16]), T.jr1[:]), (50.0, 0, 0, 256))},
+           ["jr1", kD16], ["D%d" % t])
+
+    for k in range(2):
+        copy(T.m0r[:, 256 * k:256 * k + 256], T.idw[:].indirect(T.smu[:, l0 + 16 * k:l0 + 16 * k + 16]), 256, ["idw", (kL16, 0)], [("m0r", k)], True)
+    km0r = [("m0r", 0), ("m0r", 1)]
+    rows0 = [pick(T.m0r[:], km0r, *la16(0)), pick(T.m0r[:], km0r, *lb16(0))]
+    V(lambda e: e.tensor_copy(D16, L[:, 128:176]), 48, ["ld_"], [kD16])
+    zl0 = small(128, "smu")[2]
+    zl = [None] + [small(32, "smu")[2] for _ in range(R)]
+    for half in range(2):
+        y, ky = scan([rows0[half]])
+        for p in range(4):
+            a = zl0 + 64 * half + 16 * p
+            ts(T.smu[:, a:a + 16], y, 4.0, down[p][0], OP.mult, OP.add, ky + [down[p][1]], [("zl", 0, half, p)])
+
+    def zoff(t, half, p, k):
+        a = zl[t] + 16 * half + 8 * k if t else zl0 + 64 * half + 16 * p + 8 * k
+        return T.smu[:, a:a + 8], ("zl", t, half, p if t == 0 else 0)
+
+    def window(t, p):
+        if t == 0:
+            return T.X0[:], ["X0"]
+        return T.F[:, SL * p:SL * p + 512 + 256 * t], [("Fx", p)] + [("Fn", s, h, p) for s in range(t) for h in range(2)]
+
+    def send(t, h):
+        qz, qs = T["qz%d" % t], T["qzs%d" % t]
+        lo, hi = 128 * h, 128 * h + 128
+
+        def call(q):
+            dst = T.cores[rank ^ STEP[t]]
+            rid, pid = topo.addr(dst)[:2]
+            every, n = topo.mask(core, dst), 2 * len(topo.engines(core, dst))
+            name = "arr%d%d" % (t, h)
+            gate("g", [("qz", t, h)], [])
+            g.remote_dma(T["lz%d" % t][:, lo:hi].bitcast(dt.uint8), qz[:, lo:hi].bitcast(dt.uint8), T.sem[name], T.sem.sent, pid, rid, every)
+            g.remote_dma(T["lzs%d" % t][:, lo:hi], qs[:, lo:hi], T.sem[name], T.sem.sent, pid, rid, every)
+            count["sent"] = count.get("sent", 0) + n
+            count[name] = n
+            writer[("lz", t, h)] = (name, n, {})
+        op({"g": (call, (300.0 + (800.0 if t + h == 0 else 0.0), 0, 0, 0))}, [("qz", t, h)], [("lz", t, h)], "send")
+
+    def operands(t):
+        for h in range(2):
+            for p in range(4):
+                (win, wk), (off, ko) = window(t, p), zoff(t, 0, p, h)
+                a = 1024 * t + 256 * p + 128 * h
+                copy(T.Ag[:, a:a + 128], win.indirect(off), 128, wk + [ko], [("A", t, h, p)], True)
+        for h in range(2):
+            lo, hi, z = 128 * h, 128 * h + 128, 1024 * t + 512 * h
+            for p in range(4):
+                (win, wk), (off, ko) = window(t, p), zoff(t, 1, p, h)
+                a = 1024 * t + 256 * p + 128 * h
+                out, in_, ag = T.Z[:, z + p:z + 512:4], win.indirect(off), T.Ag[:, a:a + 128]
+                op({"v": (lambda e, out=out, in_=in_, ag=ag: e.tensor_tensor(out, in_, ag, OP.add), (50.0, 0, 128, 0))},
+                   wk + [ko, ("A", t, h, p)], [("Z", t, h, p)])
+            V(lambda e, lo=lo, hi=hi, z=z: e.quantize_mx(T["qz%d" % t][:, lo:hi], T["qzs%d" % t][:, lo:hi], T.Z[:, z:z + 512]), 150,
+              [("Z", t, h, p) for p in range(4)], [("qz", t, h)])
+            send(t, h)
+
+    def bank(k):
+        return T.ps[:, 512 * k:512 * k + 128]
+
+    def mm(k, lq, ls, rq, rs, r):
+        op({"t": (lambda e: e.matmul_mx(bank(k), lq, ls, rq, rs, True, True), (0.0, 150, 0, 0))}, r, [("bk", k)])
+
+    s1 = [[small(1) for _ in range(2)] for _ in range(R)]
+    s2 = [[small(1) for _ in range(2)] for _ in range(R)]
+
+    def layer(t, h):
+        lo, hi, z = 128 * h, 128 * h + 128, 1024 * t + 512 * h
+        for b in range(4):
+            mm(b, T.wq[:, 128 * b:128 * b + 128], T.wqs[:, 128 * b:128 * b + 128], T["lz%d" % t][:, lo:hi], T["lzs%d" % t][:, lo:hi], ["wq", ("lz", t, h)])
+        for b in range(4):
+            out = T.Hb[:, z + b:z + 512:4]
+            op({"v": (lambda e, b=b, out=out: e.tensor_scalar(out, bank(b), 0.0, 0.015625, OP.max, OP.mult), (0.0, 128, 0, 0)),
+                "s": (lambda e, b=b, out=out: e.activation(out, bank(b), AF.Relu, scale=0.015625), (0.0, 128, 0, 0))}, [("bk", b)], [("H", t, h, b)])
+        V(lambda e: e.quantize_mx(T["qh%d" % t][:, lo:hi], T["qhs%d" % t][:, lo:hi], T.Hb[:, z:z + 512]), 150, [("H", t, h, b) for b in range(4)], [("qh", t, h)])
+
+    def scores(t, h):
+        lo, hi = 128 * h, 128 * h + 128
+        q, s = T["qh%d" % t][:, lo:hi], T["qhs%d" % t][:, lo:hi]
+        bs, bd = ((4, 5), (6, 7, 4, 5)) if h == 0 else ((0, 1), (2, 3, 6, 7))
+        for k in range(2):
+            mm(bs[k], T.up[:, 128 * k:128 * k + 128], T.ups[:, 128 * k:128 * k + 128], q, s, ["up", "ups", ("qh", t, h)])
+        for k, name, out, sm in ((0, "sgw", T.sgw[:, 272 * t + 1 + lo:272 * t + 1 + hi], s1[t][h]), (1, "sg2", T.sg2[:, 256 * t + lo:256 * t + hi], s2[t][h])):
+            op({"s": (lambda e, k=k, out=out, sm=sm: e.activation(out, bank(bs[k]), AF.Sign, bias=eps, accum_out=sm[0]), (20.0, 128, 0, 0))},
+               [("bk", bs[k]), keps], [(name, t, h), sm[1]])
+        for b in range(4):
+            mm(bd[b], T.eq[:, 128 * b:128 * b + 128], T.eqs[:, 128 * b:128 * b + 128], q, s, [("eq", b), ("qh", t, h)])
+            a = SL * b + 512 + 256 * t + lo
+            copy(T.F[:, a:a + 128], bank(bd[b]), 128, [("bk", bd[b])], [("Fn", t, h, b)], False)
+
+    def flags(c):
+        return T.d1[:, 1536 * c + 45:1536 * c + 1534:48]
+
+    def older(c, n=32):
+        a = 1536 * c + 61
+        return T.d1[:, a:a + 48 * n - 47:48]
+
+    def backed(c):
+        return T.d1[:, 1536 * c + 77:1536 * c + 1566:48]
+
+    def result(c, k=None):
+        return T.rs[:, 96 * c + 2:96 * c + 96:3] if k is None else T.rs[:, 96 * c + 48 * k + 2:96 * c + 48 * k + 48:3]
+
+    def kres(c):
+        return [("rs", c, 0), ("rs", c, 1)]
+
+    V(lambda e: e.tensor_copy(older(0, 96), low), 96, [klow], [("old", 0), ("old", 1), ("old", 2)])
+    for t, cs in ((1, (0,)), (2, (1, 3))):
+        y, ky = scan([pick(T.m0r[:], km0r, *l) for l in (la16(t), lb16(t))])
+        for c in cs:
+            ts(backed(c), y, mcol, 1.0 / UNIT, OP.add, OP.mult, ky + [kmcol], [("bak", c, 0), ("bak", c, 1)])
+    for c in (2, 4):
+        ts(backed(c), L[:, 0:32], float(-SL), 1.0 / UNIT, OP.add, OP.mult, ["lists"], [("bak", c, 0), ("bak", c, 1)])
+
+    def new(c, t, y, ky):
+        ts(T.d0[:, 96 * c + 1:96 * c + 96:3], y, slot[t][0], 1.0 / UNIT, OP.add, OP.mult, ky + [slot[t][1], "d0"], [("n", c)])
+
+    def where(c, t, rows):
+        y, ky = scan(rows)
+        o, ko, oa = small(32, "smu")
+        ts(o, y, mlift, None, OP.add, None, ky + [kmlift], [ko])
+        if c is not None:
+            new(c, t, y, ky)
+        return oa, ko
+
+    def ident(t):
+        return [(T.Dd[:, 512 * t + 256 * k:512 * t + 256 * k + 256], ["D%d" % t]) for k in range(2)]
+
+    def find(t, l):
+        return [pick(T.Dd[:, 512 * t:512 * t + 512], ["D%d" % t], *l2) for l2 in (la16(l), lb16(l))]
+
+    rk = [small(1) for _ in range(R)]
+
+    def limit(t):
+        kb, kkb, _ = small(32)
+        kt, kkt, ka = small(32)
+        c8, kc8, _ = small(12)
+        own, kown, _ = small(1)
+        ts(kb, fr8, s2[t][0][0], s2[t][1][0], OP.add, OP.add, [kfr8, s2[t][0][1], s2[t][1][1]], [kkb])
+        V(lambda e: e.transpose(kt, kb), 32, [kkb], [kkt])
+        ts(own, gfr, s1[t][0][0], s1[t][1][0], OP.add, OP.add, [kgfr, s1[t][0][1], s1[t][1][1]], [kown])
+        op({"s": (lambda e: e.activation(c8, T.smf[:, ka:ka + 12], AF.Sign, bias=own, scale=-1.0, accum_out=rk[t][0]), (20.0, 64, 0, 0))},
+           [kkt, kown], [kc8, rk[t][1]])
+
+    def limits(c, t):
+        out, col = T.d0[:, 96 * c + 2:96 * c + 96:3], rk[t][0]
+        op({"v": (lambda e: e.tensor_scalar(out, zero, col, None, OP.add), (0.0, 64, 0, 0)),
+            "s": (lambda e: e.activation(out, zero, AF.Identity, bias=col), (0.0, 64, 0, 0))}, [kzero, rk[t][1], "d0"], [("lim", c)])
+
+    def merge(c, t, off):
+        oa, ko = off
+        win, wk = T.sgw[:, 272 * t:272 * t + 257], [("pad", t), ("sgw", t, 0), ("sgw", t, 1), khalf1, ko]
+        limits(c, t)
+        parts = 2 if c in SPLIT else 1
+        w = 256 // parts
+        for k in range(2):
+            i = used["gx"]
+            used["gx"] = i + 1
+            row = T.gx[:, 256 * i:256 * i + 256]
+            for d in range(parts):
+                o = oa + 16 * k + 8 * d
+                out, in_ = T.gx[:, 256 * i + w * d:256 * i + w * d + w], win.indirect(T.smu[:, o:o + 16 // parts])
+                op({"v": (lambda e, out=out, in_=in_: e.tensor_scalar(out, in_, 0.5, half1, OP.mult, OP.add), (50.0, 0, w, 0)),
+                    "s": (lambda e, out=out, in_=in_: e.activation(out, in_, AF.Identity, bias=half1, scale=0.5), (65.0, 0, w, 0))}, wk, [("gx", i, d)])
+            a = 1536 * c + 768 * k
+            V(lambda e, a=a, row=row: e.tensor_tensor_scan(T.d1[:, a:a + 768:3], T.st[:, 256:512], row, 0.0, OP.add, OP.max),
+              128, [("gx", i, d) for d in range(parts)] + [("st", 256)], [("flag", c, k)])
+        for k in range(2):
+            a, b = 1536 * c + 768 * k + 45, 96 * c + 48 * k
+            V(lambda e, a=a, b=b: e.tensor_tensor_scan(T.rs[:, b:b + 48], T.d0[:, b:b + 48], T.d1[:, a:a + 753:16], 0.0, OP.min, OP.max),
+              48, [("flag", c, k), ("old", c), ("bak", c, k), ("n", c), ("lim", c), "d0"], [("rs", c, k)])
+
+    def merge_rows(c, t, rows):
+        y, ky = scan(rows)
+        limits(c, t)
+        new(c, t, y, ky)
+        ts(flags(c), y, mlift, None, OP.add, None, ky + [kmlift], [("flag", c, 0), ("flag", c, 1)])
+        a, b = 1536 * c + 45, 96 * c
+        V(lambda e: e.tensor_tensor_scan(T.rs[:, b:b + 96], T.d0[:, b:b + 96], T.d1[:, a:a + 1521:16], 0.0, OP.min, OP.max),
+          96, [("flag", c, 0), ("flag", c, 1), ("old", c), ("bak", c, 0), ("bak", c, 1), ("n", c), ("lim", c), "d0"], kres(c))
+
+    def settle(c, t, off):
+        merge(c, t, off)
+        for half in range(2):
+            a = zl[t + 1] + 16 * half
+            ts(T.smu[:, a:a + 16], result(c, half), UNIT, float(SL), OP.mult, OP.add, [("rs", c, half)], [("zl", t + 1, half, 0)])
+
+    def before(c, b):
+        V(lambda e: e.tensor_copy(older(c), result(b)), 32, kres(b), [("old", c)])
+
+    inverse(0)
+    operands(0)
+    w01 = where(0, 0, find(0, 1))
+    for p in range(4):
+        out, in_ = T.F[:, SL * p:SL * p + 512], T.X0[:, p:2048:4]
+        op({"g": (lambda e, out=out, in_=in_: e.affine_select(out, in_, [[0, 512]], OP.is_equal, 0.0, 0, 0), (170.0, 1024, 0, 0)),
+            "v": (lambda e, out=out, in_=in_: e.tensor_copy(out, in_), (0.0, 256, 0, 0))}, ["X0"], [("Fx", p)])
+    V(lambda e: e.quantize_mx(T.uq[:], T.uqs[:], T.uin[:]), 150, ["uin"], ["uq"])
+    op({"v": (lambda e: e.tensor_copy(T.up[:].bitcast(dt.uint32), T.uq[:].bitcast(dt.uint32).indirect(U16)), (50.0, 0, 256, 0))},
+       ["uq", (kU16, 0), (kU16, 1)], ["up"])
+    copy(T.ups[:], T.uqs[:].indirect(U16), 256, ["uq", (kU16, 0), (kU16, 1)], ["ups"], True)
+    for b in range(4):
+        V(lambda e, b=b: e.quantize_mx(T.eq[:, 128 * b:128 * b + 128], T.eqs[:, 128 * b:128 * b + 128], T.ez[:, 4 - b:516 - b]), 150, ["ez"], [("eq", b)])
+    layer(0, 0)
+    scores(0, 0)
+    layer(0, 1)
+    scores(0, 1)
+    limit(0)
+    settle(0, 0, w01)
+
+    operands(1)
+    inverse(1)
+    w12, w0 = where(3, 1, find(1, 2)), where(None, 0, ident(0))
+    layer(1, 0)
+    scores(1, 0)
+    tt(T.val[:, 1:257], T.sgw[:, 1:257], T.jr1[:], OP.mult, [("sgw", 0, 0), ("sgw", 0, 1), "jr1"], ["val"], 256)
+    regs = [pick(T.val[:, 0:257], ["val", ("pad", R)], T.smu[:, w0[0] + 16 * k:w0[0] + 16 * k + 16], w0[1]) for k in range(2)]
+    g0 = 256 * regs[0][1][0][1]
+    merge_rows(1, 0, [pick(T.gx[:, g0:g0 + 512], regs[0][1] + regs[1][1], *l) for l in (la16(2), lb16(2))])
+    before(3, 1)
+    layer(1, 1)
+    scores(1, 1)
+    limit(1)
+    settle(3, 1, w12)
+
+    operands(2)
+    inverse(2)
+    w1, w2 = [where(c, t, ident(t)) for c, t in ((4, 1), (5, 2))]
+    merge_rows(2, 0, regs)
+    before(4, 2)
+    merge(4, 1, w1)
+    before(5, 4)
+    gm, kgm, _ = small(32)
+    affine(gm, result(2), -1.0, 0.0, kres(2), [kgm])
+    V(lambda e: e.quantize_mx(T.vq[:], T.vqs[:], T.vin[:]), 150, ["vin"], ["vq"])
+    layer(2, 0)
+    scores(2, 0)
+    layer(2, 1)
+    scores(2, 1)
+    limit(2)
+    ts(backed(5), gm, rk[2][0], -1.0, OP.max, OP.mult, [kgm, rk[2][1]], [("bak", 5, 0), ("bak", 5, 1)])
+    settle(5, 2, w2)
+
+    def store(q, sem, pairs, r, w):
+        op({q: (lambda q: dmas(q, sem, pairs, r, w), (60.0 * len(pairs), 0, 0, 0))}, r, w, "dma")
+        ops[-1]["busy"] = 320.0 if len(pairs) == 1 else 150.0
+
+    for c in range(4):
+        lo, hi = 128 * c, 128 * c + 128
+        for p in range(4):
+            (win, wk), (off, ko) = window(3, p), zoff(3, c // 2, p, c % 2)
+            copy(T.Tt[:, 512 * c + p:512 * c + 512:4], win.indirect(off), 128, wk + [ko], [("T", c, p)], True)
+        V(lambda e, lo=lo, hi=hi: e.quantize_mx(T.oq[:, lo:hi], T.oqs[:, lo:hi], T.Tt[:, 4 * lo:4 * hi]), 150, [("T", c, p) for p in range(4)], [("oq", c)])
+        mm(4 + c, T.vq[:], T.vqs[:], T.oq[:, lo:hi], T.oqs[:, lo:hi], ["vq", ("oq", c)])
+        copy(T.yo[:, lo:hi], bank(4 + c), 128, [("bk", 4 + c)], [("yo", c)], False)
+        store("y", "so%d" % c, [(T.oc[:, 4 * lo:4 * hi], T.oq[:, lo:hi].bitcast(dt.uint8))], [("oq", c)], [("oc", c)])
+        store("y", "sy%d" % c, [(T.y[:, lo:hi], T.yo[:, lo:hi])], [("yo", c)], [("y", c)])
+    store("s", "sos", [(T.osc[4 * k:4 * k + 4, :], T.oqs[32 * k:32 * k + 4, :]) for k in range(4)], [("oq", c) for c in range(4)], ["osc"])
+    pl, kpl, _ = small(32)
+    ot, kot, oa = small(32)
+    affine(pl, result(5), UNIT, float(SL), kres(5), [kpl])
+    V(lambda e: e.transpose(ot, pl), 32, [kpl], [kot])
+    store("y", "som", [(T.om[k:8:2, :], T.smf[:, oa + 16 * k:oa + 16 * k + 16]) for k in range(2)], [kot], ["om"])
+
+    if "order" not in PLAN:
+        PLAN["order"] = make_plan(ops, ready)
+    for i, q in PLAN["order"]:
+        emit(ops[i], q)
+    for s in SEMAPHORES:
+        if known["g"].get(s, 0) < count.get(s, 0):
+            g.wait_ge(T.sem[s], count[s])

@@ -1,21 +1,20 @@
-import math
-import numpy as np
-from concourse.bass import DstId, RemoteDMATransfer
-from concourse.mybir import dt, AluOpType, AxisListType, ActivationFunctionType
+from concourse.mybir import dt, AluOpType, ActivationFunctionType
 
 OP = AluOpType
 AF = ActivationFunctionType
 R = 3
 STEP = [1, 2, 4]
-LIFT = 1024
+LIFT = 1536
+DEEP = -8192
 SL = 1280
-UNIT = 2048.0
 HALF = "float16"
-SPLIT = (0, 3, 5)
-COSTS = [(1.0, 160.0, 1.5, 3.5, 1900.0, 140.0), (1.0, 280.0, 1.3, 3.0, 2200.0, 190.0), (1.2, 120.0, 1.8, 4.5, 1800.0, 170.0),
-         (0.85, 220.0, 1.5, 3.5, 2500.0, 220.0)]
-TRIES, HEAT = 16000, 12.0
-PLAN = {}
+NS = 4
+TCUT = (128, 256, 128)
+OCUT = (1, 2, 1)
+YCUT = (1, 2, 1)
+ORDER = """
+10v 2g 1g 32v 0g 33v 15v 14v 29v 21v 17v 12v 16v 22s 18v 23s 4g 26s 19v 7s 30g 35v 5v 11g 25s 3g 8g 38v 37v 41v 40s 9g 39v 20s 34v 42v 43s 13v 45v 24s 27s 36v 47v 6g 50v 48v 49v 52v 46v 53v 54v 72s 99g 44v 73s 51v 80v 71s 81v 74s 79v 75s 82v 77s 85v 76s 83v 78s 67v 84g 55s 86v 87v 61s 68v 88v 62s 69v 56s 89v 100v 90g 57v 70v 102s 97g 31v 92s 58v 194v 103v 91s 104v 59v 60v 101v 98g 94v 106v 109t 93v 107t 108t 113s 110t 111s 112s 130t 116y 114s 129t 96g 132t 134s 115v 131t 133s 185v 136s 117t 135s 118t 95v 121t 119s 123t 137v 120s 186v 122s 138t 124s 139t 105v 142t 140s 187v 148t 141s 125t 155s 146t 152v 144t 150v 127t 158v 156s 151v 159s 188v 153s 157v 149s 160v 147s 154v 126s 161v 219v 143s 163v 162v 128s 164v 145s 167v 165s 195v 166s 175v 168s 173v 169s 174v 170s 176v 171s 179v 177v 172s 180v 190s 178g 181v 182v 28s 189s 196v 183v 218v 184g 192v 64v 220s 191v 221v 199t 197t 198t 203s 200t 201v 193v 223v 204s 202s 222s 205v 228t 229t 230t 232s 231t 233v 207t 234s 284v 212t 235s 206t 210t 209s 236v 213s 211s 63v 225v 208s 237t 238t 216t 224v 294v 239s 243t 289v 240s 247t 65v 214t 254s 226v 241t 255v 245t 258s 249v 227v 251v 257s 250v 256v 288v 252s 246s 260v 259v 244s 253v 242s 262v 248s 261v 215s 263v 217s 265v 264s 290v 267s 273v 272v 266s 275v 268s 274v 269s 278v 270s 276v 271s 279v 277g 301s 280v 281v 299s 66v 282v 295v 285v 283g 300v 286v 302v 307v 287v 296v 308t 291v 311t 309t 310t 315s 312s 314s 313s 332t 316v 331t 329t 336v 330t 335s 297v 317t 334s 333v 321t 292v 318t 319s 323t 337v 322s 320s 305v 298v 303v 339t 324v 338t 304v 325t 341s 293v 348t 306v 340s 327t 344t 350v 326s 346t 356v 355s 342t 352v 358s 351v 359v 345s 357v 353s 343s 360v 349s 361v 354v 347s 363v 328s 362v 364v 366v 367s 368v 365s 396v 373s 370v 372s 377v 397v 369v 371s 389y 378t 398y 375v 379s 376s 380v 392y 383v 374s 381t 390y 384t 382s 386v 385s 391y 395s 387t 393y 388v 394y
+"""
 
 SCRATCH = {
     "Lst": ("sbuf", [128, 176], "int32"),
@@ -27,22 +26,20 @@ SCRATCH = {
     "Tt": ("sbuf", [128, 2048], "bfloat16"),
     "uin": ("sbuf", [128, 512], "bfloat16"),
     "vin": ("sbuf", [128, 512], "bfloat16"),
-    "ones": ("sbuf", [128, 520], "bfloat16"),
-    "ez": ("sbuf", [128, 520], "bfloat16"),
-    "sw": ("sbuf", [128, 32], "bfloat16"),
-    "st": ("sbuf", [128, 512], "bfloat16"),
+    "ez": ("sbuf", [128, 528], "bfloat16"),
+    "sw": ("sbuf", [128, 16], "bfloat16"),
+    "st": ("sbuf", [128, 256], "bfloat16"),
     "idw": ("sbuf", [128, 512], "bfloat16"),
     "m0r": ("sbuf", [128, 512], "bfloat16"),
-    "jr1": ("sbuf", [128, 256], "bfloat16"),
+    "jr": ("sbuf", [128, 512], "bfloat16"),
     "Dd": ("sbuf", [128, 1536], "bfloat16"),
-    "sgw": ("sbuf", [128, 3 * 272], "bfloat16"),
-    "val": ("sbuf", [128, 272], "bfloat16"),
+    "sgw": ("sbuf", [128, 4 * 272], "bfloat16"),
     "sg2": ("sbuf", [128, 3 * 256], "bfloat16"),
     "gx": ("sbuf", [128, 256 * 24], "bfloat16"),
-    "gy": ("sbuf", [128, 256 * 20], HALF),
-    "d1": ("sbuf", [128, 12 * 768 + 64], HALF),
-    "d0": ("sbuf", [128, 6 * 96], "float32"),
-    "rs": ("sbuf", [128, 6 * 96], "float32"),
+    "gy": ("sbuf", [128, 256 * 12], HALF),
+    "d0": ("sbuf", [128, 8 * 768 + 64], HALF),
+    "d1": ("sbuf", [128, 8 * 768 + 64], HALF),
+    "rs": ("sbuf", [128, 8 * 48], "float32"),
     "smi": ("sbuf", [128, 320], "int32"),
     "smf": ("sbuf", [128, 2560], "float32"),
     "smu": ("sbuf", [128, 1280], "uint16"),
@@ -60,158 +57,9 @@ for _t in range(R):
         SCRATCH["%s%d" % (_n, _t)] = ("sbuf", [128, 256], "float8_e4m3fn_x4")
         SCRATCH["%ss%d" % (_n, _t)] = ("sbuf", [128, 256], "uint8")
 ENG = {"v": "ve", "s": "ac", "t": "pe", "g": "gp"}
-LOADS = ["lm", "lx", "ll", "lu", "lw", "lv"]
+LOADS = ["lm", "la", "lb", "lx", "ll", "lu", "lw", "lv"]
 STORES = ["so0", "so1", "so2", "so3", "sy0", "sy1", "sy2", "sy3", "som", "sos"]
 SEMAPHORES = ["ve", "ac", "pe", "gp", "sent"] + ["arr%d%d" % (t, h) for t in range(R) for h in range(2)] + LOADS + STORES
-MAIN = ("zl", "Fn", "A", "Z", "qz", "lz", "H", "qh", "flag", "lim", "T", "oq", "yo")
-
-
-def price(o, q, c):
-    fix, cyc, gat, sca = o["q"][q][1]
-    return c[5] if q == "t" else fix + c[0] * (cyc + c[2] * gat + c[3] * sca)
-
-
-def make_plan(ops, ready):
-    n = len(ops)
-    pred, succ, wrote, read = [[] for _ in ops], [[] for _ in ops], {}, {}
-    for i, o in enumerate(ops):
-        p = {}
-        for k in o["w"]:
-            for j in read.get(k, []) + ([wrote[k]] if k in wrote else []):
-                p[j] = False
-        for k in o["r"]:
-            if k in wrote:
-                p[wrote[k]] = True
-        for k in o["r"]:
-            read.setdefault(k, []).append(i)
-        for k in o["w"]:
-            wrote[k], read[k] = i, []
-        p.pop(i, None)
-        pred[i] = sorted(p.items())
-        for j in p:
-            succ[j].append(i)
-    first = [max([ready.get(k, 0.0) for k in o["r"]] + [0.0]) for o in ops]
-    lag = [[c[4] if o["kind"] == "send" else 1700.0 if o["kind"] == "dma" else 0.0 for o in ops] for c in COSTS]
-    cost = [[{q: price(o, q, c) for q in o["q"]} for o in ops] for c in COSTS]
-    busy = [o.get("busy", 0.0) for o in ops]
-    weight = [0.3 / n if o["w"][0][0] in MAIN else 0.0 for o in ops]
-    rank = [0.0] * n
-    for i in range(n - 1, -1, -1):
-        rank[i] = min(cost[0][i].values()) + lag[0][i] + max([COSTS[0][1] + rank[j] for j in succ[i]] + [0.0])
-
-    def greedy():
-        free, fin, start, where, left = {}, [0.0] * n, [0.0] * n, [""] * n, [len(p) for p in pred]
-        cand = [i for i in range(n) if not left[i]]
-        for _ in range(n):
-            best = []
-            for i in cand:
-                opt = []
-                for q in ops[i]["q"]:
-                    t = max(first[i], free.get(q, 0.0))
-                    for j, raw in pred[i]:
-                        t = max(t, fin[j] + COSTS[0][1] if raw or where[j] != q else start[j])
-                    opt.append((t + cost[0][i][q] + (60.0 if q == "v" and len(ops[i]["q"]) > 1 else 0.0), t, q))
-                best.append((min(opt), i))
-            soon = min(b[0][1] for b in best)
-            (_, t, q), i = max((b for b in best if b[0][1] <= soon + 120.0), key=lambda b: (rank[b[1]], -b[1]))
-            start[i], where[i] = t, q
-            free[q] = t + cost[0][i][q]
-            fin[i] = free[q] + lag[0][i]
-            cand.remove(i)
-            for j in succ[i]:
-                left[j] -= 1
-                if not left[j]:
-                    cand.append(j)
-        return sorted(range(n), key=lambda i: (start[i], i)), where
-
-    free, start, fin = [None] * len(COSTS), [None] * len(COSTS), [None] * len(COSTS)
-
-    def span(seq, where, a):
-        total = 0.0
-        for k, c in enumerate(COSTS):
-            wake, ck, lk, snap, sk, fk = c[1], cost[k], lag[k], free[k][:a + 1], start[k], fin[k]
-            f5, end, late = snap[a]
-            f5 = dict(f5)
-            for i in seq[a:]:
-                q = where[i]
-                t = first[i]
-                f = f5[q]
-                if f > t:
-                    t = f
-                for j, raw in pred[i]:
-                    f = fk[j] + wake if raw or where[j] != q else sk[j]
-                    if f > t:
-                        t = f
-                sk[i] = t
-                f = t + ck[i][q]
-                f5[q] = f
-                if busy[i]:
-                    f = max(f + lk[i], f5["e"]) + busy[i]
-                    f5["e"] = f
-                    f += 500.0
-                else:
-                    f += lk[i]
-                fk[i] = f
-                late += f * weight[i]
-                if f > end:
-                    end = f
-                snap.append((dict(f5), end, late))
-            free[k] = snap
-            total += end + late
-        return total
-
-    for k in range(len(COSTS)):
-        free[k], start[k], fin[k] = [({"v": 0.0, "s": 0.0, "t": 0.0, "g": 0.0, "y": 0.0, "e": 0.0}, 0.0, 0.0)], [0.0] * n, [0.0] * n
-    seq, where = greedy()
-    seed = [12345]
-
-    def draw(m):
-        seed[0] = (seed[0] * 1103515245 + 12345) % 2147483648
-        return (seed[0] >> 8) % m
-
-    now = span(seq, where, 0)
-    kept = (now, list(seq), list(where))
-    pos = [0] * n
-    for k, i in enumerate(seq):
-        pos[i] = k
-    both = [i for i in range(n) if len(ops[i]["q"]) > 1]
-    for it in range(TRIES):
-        heat = HEAT * (1.0 - it / TRIES) + 0.1
-        flip = draw(6) == 0
-        i = both[draw(len(both))] if flip else draw(n)
-        a = b = pos[i]
-        if not flip:
-            lo = max([pos[j] for j, _ in pred[i]] + [-1]) + 1
-            hi = min([pos[j] for j in succ[i]] + [n]) - 1
-            if hi <= lo:
-                continue
-            if draw(3):
-                d = 1 if draw(2) else -1
-                b = a + d
-                while lo <= b <= hi and where[seq[b]] != where[i]:
-                    b += d
-            else:
-                b = max(lo, a - 60) + draw(min(hi, a + 60) - max(lo, a - 60) + 1)
-            if b == a or b < lo or b > hi:
-                continue
-        old = (where[i], list(free), [list(s) for s in start], [list(s) for s in fin])
-        if flip:
-            where[i] = [q for q in sorted(ops[i]["q"]) if q != where[i]][0]
-        else:
-            seq.insert(b, seq.pop(a))
-        new = span(seq, where, min(a, b))
-        if new <= now or draw(10000) < 10000 * math.exp((now - new) / heat):
-            now = new
-            for k in range(min(a, b), max(a, b) + 1):
-                pos[seq[k]] = k
-            if now < kept[0]:
-                kept = (now, list(seq), list(where))
-        else:
-            where[i] = old[0]
-            seq.insert(a, seq.pop(b))
-            for k in range(len(COSTS)):
-                free[k], start[k], fin[k] = old[1][k], old[2][k], old[3][k]
-    return [(i, kept[2][i]) for i in kept[1]]
 
 
 def rank_program(g, core, T, topo):
@@ -238,7 +86,7 @@ def rank_program(g, core, T, topo):
         own = ENG.get(q)
         evs = [writer[k] for k in r]
         for k in w:
-            if k in writer and writer[k][0] != own:
+            if k in writer and (writer[k][0] != own or q != "t"):
                 evs.append(writer[k])
             evs += [e for e in readers.get(k, {}).values() if e[0] != own]
         for e in sorted(evs, key=lambda e: -e[1]):
@@ -259,7 +107,7 @@ def rank_program(g, core, T, topo):
         note((sem, count[sem], dict(known[q])), r, w)
 
     def emit(o, q):
-        call = o["q"][q][0]
+        call = o["q"][q]
         if o["kind"] != "call":
             call(q)
             return
@@ -279,151 +127,146 @@ def rank_program(g, core, T, topo):
         used[buf] = a + n
         return T[buf][:, a:a + n], (buf, a), a
 
-    def V(call, n, r=(), w=()):
-        op({"v": (call, (0.0, max(64, n), 0, 0))}, r, w)
+    def V(call, r=(), w=()):
+        op({"v": call}, r, w)
 
-    def G(call, n, r=(), w=()):
-        op({"g": (call, (150.0, 2 * n, 0, 0))}, r, w)
+    def G(call, r=(), w=()):
+        op({"g": call}, r, w)
 
-    def ts(out, in0, s1, s2, op0, op1, r, w, n=32):
+    def ts(out, in0, s1, s2, op0, op1, r, w):
         if op1 is None:
-            V(lambda e: e.tensor_scalar(out, in0, s1, s2, op0), n, r, w)
+            V(lambda e: e.tensor_scalar(out, in0, s1, s2, op0), r, w)
         else:
-            V(lambda e: e.tensor_scalar(out, in0, s1, s2, op0, op1), n, r, w)
+            V(lambda e: e.tensor_scalar(out, in0, s1, s2, op0, op1), r, w)
 
-    def tt(out, a, b, o, r, w, n=64):
-        V(lambda e: e.tensor_tensor(out, a, b, o), n, r, w)
+    def tt(out, a, b, o, r, w):
+        V(lambda e: e.tensor_tensor(out, a, b, o), r, w)
 
-    def copy(out, in_, n, r, w, gather):
-        c = ((50.0, 0, n, 0), (65.0, 0, n, 0)) if gather else ((0.0, max(64, n), 0, 0), (0.0, max(64, n), 0, 0))
-        op({"v": (lambda e: e.tensor_copy(out, in_), c[0]), "s": (lambda e: e.activation(out, in_, AF.Copy), c[1])}, r, w)
+    def copy(out, in_, r, w):
+        op({"v": lambda e: e.tensor_copy(out, in_), "s": lambda e: e.activation(out, in_, AF.Copy)}, r, w)
 
-    def affine(out, in_, scale, bias, r, w, n=32):
-        op({"v": (lambda e: e.tensor_scalar(out, in_, scale, bias, OP.mult, OP.add), (0.0, max(64, n), 0, 0)),
-            "s": (lambda e: e.activation(out, in_, AF.Copy, bias=bias, scale=scale), (0.0, max(64, n), 0, 0))}, r, w)
+    def affine(out, in_, scale, bias, r, w):
+        op({"v": lambda e: e.tensor_scalar(out, in_, scale, bias, OP.mult, OP.add),
+            "s": lambda e: e.activation(out, in_, AF.Copy if isinstance(bias, float) else AF.Identity, bias=bias, scale=scale)}, r, w)
 
-    def fill(out, v, n, cycles, key):
-        op({"v": (lambda e: e.memset(out, float(v)), (0.0, cycles, 0, 0)),
-            "g": (lambda e: e.iota(out, [[0, n]], v, 0, allow_small_or_imprecise_dtypes=True), (150.0, 2 * n, 0, 0))}, [], [key])
+    def fill(out, v, n, key):
+        op({"v": lambda e: e.memset(out, float(v)),
+            "g": lambda e: e.iota(out, [[0, n]], v, 0, allow_small_or_imprecise_dtypes=True)}, [], [key])
 
-    def pick(win, wkeys, off, okey):
+    def pick(win, wkeys, off, okey, parts=1, scale=None, bias=None):
         i = used["gx"]
         used["gx"] = i + 1
-        out = T.gx[:, 256 * i:256 * i + 256]
-        copy(out, win.indirect(off), 256, list(wkeys) + [okey], [("gx", i)], True)
-        return out, [("gx", i)]
+        w, n = 256 // parts, 16 // parts
+        for d in range(parts):
+            out, in_ = T.gx[:, 256 * i + w * d:256 * i + w * d + w], win.indirect(T.smu[:, off + n * d:off + n * d + n])
+            if scale is None:
+                copy(out, in_, list(wkeys) + [okey], [("gx", i, d)])
+            else:
+                affine(out, in_, scale, bias, list(wkeys) + [okey], [("gx", i, d)])
+        return T.gx[:, 256 * i:256 * i + 256], [("gx", i, d) for d in range(parts)]
+
+    def lifted(out, row, keys, w):
+        V(lambda e: e.tensor_tensor_scan(out, T.st[:], row, 0.0, OP.add, OP.max), list(keys) + ["st"], w)
 
     def scan(rows):
         first = used["gy"]
         for row, keys in rows:
             i = used["gy"]
             used["gy"] = i + 1
-            V(lambda e, i=i, row=row: e.tensor_tensor_scan(T.gy[:, 256 * i:256 * i + 256], T.st[:, 0:256], row, 0.0, OP.add, OP.max),
-              128, keys + [("st", 0)], [("gy", i)])
+            lifted(T.gy[:, 256 * i:256 * i + 256], row, keys, [("gy", i)])
         return T.gy[:, 256 * first + 15:256 * first + 256 * len(rows):16], [("gy", first + k) for k in range(len(rows))]
 
     L = T.Lst
     dmas("y", "lm", [(L[:, 0:32], T.m[:])], w=["m_"])
-    dmas("s", "lm", [(L[:, 80:128], T.lb[:])], w=["lb_"])
-    dmas("y", "lm", [(L[:, 32:80], T.la[:])], w=["lists"])
-    writer["lists"] = ("lm", 48, {})
-    dmas("s", "ll", [(L[:, 128:176], T.ld[:])], w=["ld_"])
+    dmas("s", "lb", [(L[:, 80:128], T.lb[:])], w=["lb_"])
+    dmas("y", "la", [(L[:, 32:80], T.la[:])], w=["la_"])
     dmas("y", "lx", [(T.X0[:], T.x[:])], w=["X0"])
+    dmas("y", "ll", [(L[:, 128:176], T.ld[:])], w=["ld_"])
     dmas("y", "lu", [(T.uin[:], T.u[:])], w=["uin"])
     dmas("y", "lw", [(T.wq[:].bitcast(dt.uint8), T.wc[:]), (T.wqs[:], T.ws[:])], w=["wq"])
-    dmas("y", "lv", [(T.vin[:], T.v[:])], w=["vin"])
-    ready = {"lists": 2300.0, "ld_": 2350.0, "X0": 4600.0, "uin": 5200.0, "wq": 6800.0, "vin": 7300.0}
 
-    vI, kvI, _ = small(32, "smi")
-    pI, kpI, _ = small(32, "smi")
-    kI, kkI, akI = small(32, "smi")
-    G(lambda e: e.iota(vI, [[-1, 32]], 512, 1), 32, w=[kvI])
-    G(lambda e: e.iota(pI, [[0, 32]], 0, 1), 32, w=[kpI])
-    G(lambda e: e.iota(T.idw[:], [[1, 512]], -256, 0, allow_small_or_imprecise_dtypes=True), 512, w=["idw"])
-    G(lambda e: e.iota(kI, [[16, 32]], 0, 0), 32, w=[kkI])
-    G(lambda e: e.iota(T.jr1[:], [[1, 256]], 1, 0, allow_small_or_imprecise_dtypes=True), 256, w=["jr1"])
+    vI, kvI, _ = small(16, "smi")
+    pI, kpI, apI = small(32, "smi")
+    kI, kkI, _ = small(8, "smi")
+    c4, kc4, _ = small(1)
+    G(lambda e: e.iota(T.idw[:, 0:256], [[1, 256]], -256, 0, allow_small_or_imprecise_dtypes=True), w=[("idw", 0)])
+    G(lambda e: e.iota(vI, [[-1, 16]], 512, 1), w=[kvI])
+    G(lambda e: e.iota(pI, [[0, 32]], 0, 1), w=[kpI])
+    G(lambda e: e.iota(kI, [[16, 8]], 0, 0), w=[kkI])
+    G(lambda e: e.iota(c4, [[0, 1]], -256, 4, allow_small_or_imprecise_dtypes=True), w=[kc4])
+    affine(T.idw[:, 256:512], T.idw[:, 0:256], 1.0, 256.0, [("idw", 0)], [("idw", 1)])
+    kidw = [("idw", 0), ("idw", 1)]
+    op({"g": lambda e: e.iota(T.jr[:, 0:256], [[1, 256]], 1, 0, allow_small_or_imprecise_dtypes=True),
+        "v": lambda e: e.tensor_scalar(T.jr[:, 0:256], T.idw[:, 0:256], 257.0, None, OP.add),
+        "s": lambda e: e.activation(T.jr[:, 0:256], T.idw[:, 0:256], AF.Copy, bias=257.0)}, [("idw", 0)], ["jr1"])
+    affine(T.jr[:, 256:512], T.idw[:, 0:256], 1.0 / 1024, 257.0 / 1024, [("idw", 0)], ["jrs"])
     eps, keps, _ = small(1)
-    zero, kzero, _ = small(32)
-    low, klow, _ = small(96)
-    fill(T.d0[:], -16, 576, 576, "d0")
-    V(lambda e: e.memset(low, -1.0), 96, w=[klow])
-    V(lambda e: e.memset(zero, 0.0), 32, w=[kzero])
     for t in range(R):
-        fill(T.Dd[:, 512 * t:512 * t + 512], 0, 512, 256, "D%d" % t)
-        V(lambda e, t=t: e.memset(T.sgw[:, 272 * t:272 * t + 1], -1.0), 1, w=[("pad", t)])
-    V(lambda e: e.memset(T.val[:, 0:1], -256.0), 1, w=[("pad", R)])
-    V(lambda e: e.memset(eps, 1e-37), 1, w=[keps])
-    vJ, kvJ, _ = small(32, "smi")
-    p15, kp15, ap15 = small(32, "smi")
+        fill(T.Dd[:, 512 * t:512 * t + 512], 0, 512, "D%d" % t)
+    fill(T.sgw[:, 0:4 * 272:272], -1, 4, "pad")
+    V(lambda e: e.memset(eps, 1e-37), w=[keps])
+    ts(T.d0[:, 13:13 + 16 * 386:16], T.idw[:, 0:386], 0.0, float(DEEP), OP.mult, OP.add, kidw, ["d0"])
+    vJ, kvJ, _ = small(16, "smi")
+    p15, kp15, ap15 = small(16, "smi")
     p7, kp7, ap7 = small(32, "smi")
-    p31, kp31, _ = small(32, "smi")
-    pg, kpg, apg = small(32, "smi")
-    s_a, ks_a, _ = small(32)
-    s_b, ks_b, _ = small(32)
+    pg, kpg, _ = small(1, "smi")
+    s_a, ks_a, _ = small(16)
+    s_b, ks_b, _ = small(16)
     r16, kr16, _ = small(16, "smu")
     ts(vJ, vI, 15, None, OP.bitwise_and, None, [kvI], [kvJ])
-    ts(p15, pI, 15, None, OP.bitwise_and, None, [kpI], [kp15])
+    ts(p15, T.smi[:, apI:apI + 16], 15, None, OP.bitwise_and, None, [kpI], [kp15])
     ts(s_a, vJ, 15, LIFT, OP.is_equal, OP.mult, [kvJ], [ks_a])
-    ts(s_b, vJ, 0, -2 * LIFT, OP.is_equal, OP.mult, [kvJ], [ks_b])
-    V(lambda e: e.tensor_copy(r16, T.smi[:, ap15:ap15 + 16]), 16, [kp15], [kr16])
+    ts(s_b, vJ, 0, DEEP, OP.is_equal, OP.mult, [kvJ], [ks_b])
+    V(lambda e: e.tensor_copy(r16, p15), [kp15], [kr16])
     tt(T.sw[:], s_a, s_b, OP.add, [ks_a, ks_b], ["sw"])
-    copy(T.st[:, 0:256], T.sw[:].indirect(r16), 256, ["sw", kr16], [("st", 0)], True)
-    op({"s": (lambda e: e.activation(T.st[:, 256:512], T.sw[:].indirect(r16), AF.Copy, scale=1.0 / LIFT), (65.0, 0, 256, 0))}, ["sw", kr16], [("st", 256)])
+    copy(T.st[:], T.sw[:].indirect(r16), ["sw", kr16], ["st"])
     lift, klift, _ = small(1)
-    last, klast, _ = small(1)
     ts(lift, T.smi[:, ap15:ap15 + 1], 15, LIFT, OP.is_lt, OP.mult, [kp15], [klift])
-    ts(last, T.smi[:, ap15:ap15 + 1], 15, 2.0, OP.is_equal, OP.subtract, [kp15], [klast])
-    half1, khalf1, _ = small(1)
-    ts(half1, last, 0.5, None, OP.add, None, [klast], [khalf1])
-    mcol, kmcol, _ = small(1)
-    ts(mcol, lift, -1.0, float(256 - SL), OP.mult, OP.add, [klift], [kmcol])
     down = []
     for p in range(4):
         down.append(small(1))
-        ts(down[p][0], lift, -4.0, float(1024 + p), OP.mult, OP.add, [klift], [down[p][1]])
-    mlift, kmlift, _ = small(1)
-    ts(mlift, lift, -1.0, None, OP.mult, None, [klift], [kmlift])
-    slot = []
+        affine(down[p][0], lift, -4.0, float(1024 + p), [klift], [down[p][1]])
+    mid = []
     for t in range(R):
-        slot.append(small(1))
-        ts(slot[t][0], lift, -1.0, float(511 + 256 * t - SL), OP.mult, OP.add, [klift], [slot[t][1]])
-    fill(T.ones[:], 1, 520, 260, "ones")
-    G(lambda e: e.affine_select(T.ez[:], T.ones[:], [[-1, 520]], OP.is_equal, 0.0, 4, 4), 520, ["ones"], ["ez"])
-    f_a, kf_a, _ = small(32)
-    f_b, kf_b, _ = small(32)
+        mid.append(small(1))
+        affine(mid[t][0], lift, -2.0, float(512 + 256 * t - LIFT // 2), [klift], [mid[t][1]])
+    base, kbase, _ = small(1)
+    ts(base, T.smi[:, ap15:ap15 + 1], 3.0, 1.0, OP.mult, OP.add, [kp15], [kbase])
+    fill(T.ez[:, 0:16], 0, 16, ("ez", 0))
+    ts(T.ez[:, 16:528], T.idw[:], c4, None, OP.is_equal, None, kidw + [kc4], [("ez", 1)])
     fr8, kfr8, _ = small(32)
     gfr, kgfr, _ = small(1)
     U16, kU16, u0 = small(16, "smu")
     ts(p7, pI, 7, None, OP.bitwise_and, None, [kpI], [kp7])
-    ts(p31, pI, 31, None, OP.bitwise_and, None, [kpI], [kp31])
-    ts(pg, pI, 4, None, OP.arith_shift_right, None, [kpI], [kpg])
-    ts(f_a, p31, 0.125, None, OP.mult, None, [kp31], [kf_a])
-    ts(f_b, p31, 8, -8192.0, OP.is_ge, OP.mult, [kp31], [kf_b])
-    tt(fr8, f_a, f_b, OP.add, [kf_a, kf_b], [kfr8])
-    ts(gfr, T.smi[:, apg:apg + 1], 0.125, None, OP.mult, None, [kpg], [kgfr])
-    V(lambda e: e.tensor_copy(T.smu[:, u0:u0 + 8], T.smi[:, akI:akI + 8]), 8, [kkI], [(kU16, 0)])
+    ts(pg, T.smi[:, apI:apI + 1], 4, None, OP.arith_shift_right, None, [kpI], [kpg])
+    ts(fr8, p7, 0.125, None, OP.mult, None, [kp7], [kfr8])
+    ts(gfr, pg, 0.125, None, OP.mult, None, [kpg], [kgfr])
+    V(lambda e: e.tensor_copy(T.smu[:, u0:u0 + 8], kI), [kkI], [(kU16, 0)])
     ts(T.smu[:, u0 + 8:u0 + 16], T.smi[:, ap7:ap7 + 8], 16, None, OP.mult, None, [kp7], [(kU16, 1)])
 
     L16, kL16, l0 = small(128, "smu")
     D16, kD16, d0 = small(48, "smu")
-    V(lambda e: e.tensor_copy(T.smu[:, l0:l0 + 32], L[:, 0:32]), 32, ["lists"], [(kL16, 0)])
-    V(lambda e: e.tensor_copy(T.smu[:, l0 + 32:l0 + 128], L[:, 32:128]), 96, ["lists"], [(kL16, 1)])
+    V(lambda e: e.tensor_copy(T.smu[:, l0:l0 + 32], L[:, 0:32]), ["m_"], [(kL16, 0)])
+    V(lambda e: e.tensor_copy(T.smu[:, l0 + 32:l0 + 128], L[:, 32:128]), ["la_", "lb_"], [(kL16, 1)])
 
     def la16(t):
-        return T.smu[:, l0 + 32 + 16 * t:l0 + 48 + 16 * t], (kL16, 1)
+        return l0 + 32 + 16 * t, (kL16, 1)
 
     def lb16(t):
-        return T.smu[:, l0 + 80 + 16 * t:l0 + 96 + 16 * t], (kL16, 1)
+        return l0 + 80 + 16 * t, (kL16, 1)
 
     def inverse(t):
-        op({"v": (lambda e: e.tensor_copy(T.Dd[:, 512 * t:512 * t + 512].indirect(T.smu[:, d0 + 16 * t:d0 + 16 * t + 16]), T.jr1[:]), (50.0, 0, 0, 256))},
-           ["jr1", kD16], ["D%d" % t])
+        n = 16 // NS
+        for k in range(NS):
+            a = d0 + 16 * t + n * k
+            V(lambda e, a=a, k=k: e.tensor_copy(T.Dd[:, 512 * t:512 * t + 512].indirect(T.smu[:, a:a + n]), T.jr[:, 16 * n * k:16 * n * (k + 1)]),
+              ["jr1", kD16], ["D%d" % t])
 
     for k in range(2):
-        copy(T.m0r[:, 256 * k:256 * k + 256], T.idw[:].indirect(T.smu[:, l0 + 16 * k:l0 + 16 * k + 16]), 256, ["idw", (kL16, 0)], [("m0r", k)], True)
+        copy(T.m0r[:, 256 * k:256 * k + 256], T.idw[:].indirect(T.smu[:, l0 + 16 * k:l0 + 16 * k + 16]), kidw + [(kL16, 0)], [("m0r", k)])
     km0r = [("m0r", 0), ("m0r", 1)]
     rows0 = [pick(T.m0r[:], km0r, *la16(0)), pick(T.m0r[:], km0r, *lb16(0))]
-    V(lambda e: e.tensor_copy(D16, L[:, 128:176]), 48, ["ld_"], [kD16])
+    V(lambda e: e.tensor_copy(D16, L[:, 128:176]), ["ld_"], [kD16])
     zl0 = small(128, "smu")[2]
     zl = [None] + [small(32, "smu")[2] for _ in range(R)]
     for half in range(2):
@@ -456,31 +299,29 @@ def rank_program(g, core, T, topo):
             count["sent"] = count.get("sent", 0) + n
             count[name] = n
             writer[("lz", t, h)] = (name, n, {})
-        op({"g": (call, (300.0 + (800.0 if t + h == 0 else 0.0), 0, 0, 0))}, [("qz", t, h)], [("lz", t, h)], "send")
+        op({"g": call}, [("qz", t, h)], [("lz", t, h)], "send")
 
     def operands(t):
         for h in range(2):
             for p in range(4):
                 (win, wk), (off, ko) = window(t, p), zoff(t, 0, p, h)
                 a = 1024 * t + 256 * p + 128 * h
-                copy(T.Ag[:, a:a + 128], win.indirect(off), 128, wk + [ko], [("A", t, h, p)], True)
+                copy(T.Ag[:, a:a + 128], win.indirect(off), wk + [ko], [("A", t, h, p)])
         for h in range(2):
             lo, hi, z = 128 * h, 128 * h + 128, 1024 * t + 512 * h
             for p in range(4):
                 (win, wk), (off, ko) = window(t, p), zoff(t, 1, p, h)
                 a = 1024 * t + 256 * p + 128 * h
-                out, in_, ag = T.Z[:, z + p:z + 512:4], win.indirect(off), T.Ag[:, a:a + 128]
-                op({"v": (lambda e, out=out, in_=in_, ag=ag: e.tensor_tensor(out, in_, ag, OP.add), (50.0, 0, 128, 0))},
-                   wk + [ko, ("A", t, h, p)], [("Z", t, h, p)])
-            V(lambda e, lo=lo, hi=hi, z=z: e.quantize_mx(T["qz%d" % t][:, lo:hi], T["qzs%d" % t][:, lo:hi], T.Z[:, z:z + 512]), 150,
+                tt(T.Z[:, z + p:z + 512:4], win.indirect(off), T.Ag[:, a:a + 128], OP.add, wk + [ko, ("A", t, h, p)], [("Z", t, h, p)])
+            V(lambda e, lo=lo, hi=hi, z=z: e.quantize_mx(T["qz%d" % t][:, lo:hi], T["qzs%d" % t][:, lo:hi], T.Z[:, z:z + 512]),
               [("Z", t, h, p) for p in range(4)], [("qz", t, h)])
             send(t, h)
 
-    def bank(k):
-        return T.ps[:, 512 * k:512 * k + 128]
+    def bank(k, n=128):
+        return T.ps[:, 512 * k:512 * k + n]
 
     def mm(k, lq, ls, rq, rs, r):
-        op({"t": (lambda e: e.matmul_mx(bank(k), lq, ls, rq, rs, True, True), (0.0, 150, 0, 0))}, r, [("bk", k)])
+        op({"t": lambda e: e.matmul_mx(bank(k), lq, ls, rq, rs, True, True)}, r, [("bk", k)])
 
     s1 = [[small(1) for _ in range(2)] for _ in range(R)]
     s2 = [[small(1) for _ in range(2)] for _ in range(R)]
@@ -488,60 +329,57 @@ def rank_program(g, core, T, topo):
     def layer(t, h):
         lo, hi, z = 128 * h, 128 * h + 128, 1024 * t + 512 * h
         for b in range(4):
-            mm(b, T.wq[:, 128 * b:128 * b + 128], T.wqs[:, 128 * b:128 * b + 128], T["lz%d" % t][:, lo:hi], T["lzs%d" % t][:, lo:hi], ["wq", ("lz", t, h)])
+            mm(4 * h + b, T.wq[:, 128 * b:128 * b + 128], T.wqs[:, 128 * b:128 * b + 128], T["lz%d" % t][:, lo:hi], T["lzs%d" % t][:, lo:hi], ["wq", ("lz", t, h)])
         for b in range(4):
             out = T.Hb[:, z + b:z + 512:4]
-            op({"v": (lambda e, b=b, out=out: e.tensor_scalar(out, bank(b), 0.0, 0.015625, OP.max, OP.mult), (0.0, 128, 0, 0)),
-                "s": (lambda e, b=b, out=out: e.activation(out, bank(b), AF.Relu, scale=0.015625), (0.0, 128, 0, 0))}, [("bk", b)], [("H", t, h, b)])
-        V(lambda e: e.quantize_mx(T["qh%d" % t][:, lo:hi], T["qhs%d" % t][:, lo:hi], T.Hb[:, z:z + 512]), 150, [("H", t, h, b) for b in range(4)], [("qh", t, h)])
+            op({"v": lambda e, b=b, out=out: e.tensor_scalar(out, bank(4 * h + b), 0.0, 0.015625, OP.max, OP.mult),
+                "s": lambda e, b=b, out=out: e.activation(out, bank(4 * h + b), AF.Relu, scale=0.015625)}, [("bk", 4 * h + b)], [("H", t, h, b)])
+        V(lambda e: e.quantize_mx(T["qh%d" % t][:, lo:hi], T["qhs%d" % t][:, lo:hi], T.Hb[:, z:z + 512]), [("H", t, h, b) for b in range(4)], [("qh", t, h)])
 
     def scores(t, h):
         lo, hi = 128 * h, 128 * h + 128
         q, s = T["qh%d" % t][:, lo:hi], T["qhs%d" % t][:, lo:hi]
-        bs, bd = ((4, 5), (6, 7, 4, 5)) if h == 0 else ((0, 1), (2, 3, 6, 7))
+        bs, bd = ((0, 1), (2, 3, 0, 1)) if h == 0 else ((4, 5), (6, 7, 2, 3))
         for k in range(2):
             mm(bs[k], T.up[:, 128 * k:128 * k + 128], T.ups[:, 128 * k:128 * k + 128], q, s, ["up", "ups", ("qh", t, h)])
         for k, name, out, sm in ((0, "sgw", T.sgw[:, 272 * t + 1 + lo:272 * t + 1 + hi], s1[t][h]), (1, "sg2", T.sg2[:, 256 * t + lo:256 * t + hi], s2[t][h])):
-            op({"s": (lambda e, k=k, out=out, sm=sm: e.activation(out, bank(bs[k]), AF.Sign, bias=eps, accum_out=sm[0]), (20.0, 128, 0, 0))},
+            op({"s": lambda e, k=k, out=out, sm=sm: e.activation(out, bank(bs[k]), AF.Sign, bias=eps, accum_out=sm[0])},
                [("bk", bs[k]), keps], [(name, t, h), sm[1]])
         for b in range(4):
             mm(bd[b], T.eq[:, 128 * b:128 * b + 128], T.eqs[:, 128 * b:128 * b + 128], q, s, [("eq", b), ("qh", t, h)])
             a = SL * b + 512 + 256 * t + lo
-            copy(T.F[:, a:a + 128], bank(bd[b]), 128, [("bk", bd[b])], [("Fn", t, h, b)], False)
+            copy(T.F[:, a:a + 128], bank(bd[b]), [("bk", bd[b])], [("Fn", t, h, b)])
 
-    def flags(c):
-        return T.d1[:, 1536 * c + 45:1536 * c + 1534:48]
-
-    def older(c, n=32):
+    def older(c, k=None):
         a = 1536 * c + 61
-        return T.d1[:, a:a + 48 * n - 47:48]
+        return T.d1[:, a:a + 1489:48] if k is None else T.d1[:, a + 768 * k:a + 768 * k + 721:48]
 
     def backed(c):
         return T.d1[:, 1536 * c + 77:1536 * c + 1566:48]
 
-    def result(c, k=None):
-        return T.rs[:, 96 * c + 2:96 * c + 96:3] if k is None else T.rs[:, 96 * c + 48 * k + 2:96 * c + 48 * k + 48:3]
+    def both(name, c):
+        return [(name, c, 0), (name, c, 1)]
 
-    def kres(c):
-        return [("rs", c, 0), ("rs", c, 1)]
+    def places(outs, y, ky, w):
+        for out, k in zip(outs, w):
+            ts(out, y, lift, 257.0, OP.subtract, OP.add, ky + [klift], k)
 
-    V(lambda e: e.tensor_copy(older(0, 96), low), 96, [klow], [("old", 0), ("old", 1), ("old", 2)])
-    for t, cs in ((1, (0,)), (2, (1, 3))):
-        y, ky = scan([pick(T.m0r[:], km0r, *l) for l in (la16(t), lb16(t))])
-        for c in cs:
-            ts(backed(c), y, mcol, 1.0 / UNIT, OP.add, OP.mult, ky + [kmcol], [("bak", c, 0), ("bak", c, 1)])
-    for c in (2, 4):
-        ts(backed(c), L[:, 0:32], float(-SL), 1.0 / UNIT, OP.add, OP.mult, ["lists"], [("bak", c, 0), ("bak", c, 1)])
+    y, ky = scan([pick(T.m0r[:], km0r, *l) for l in (la16(1), lb16(1))])
+    places([older(0), backed(0)], y, ky, [both("old", 0), [("bak", 0)]])
+    y, ky = scan([pick(T.m0r[:], km0r, *l) for l in (la16(2), lb16(2))])
+    places([backed(1)], y, ky, [[("bak", 1)]])
+    ts(backed(2), L[:, 0:32], 1.0, None, OP.add, None, ["m_"], [("bak", 2)])
 
-    def new(c, t, y, ky):
-        ts(T.d0[:, 96 * c + 1:96 * c + 96:3], y, slot[t][0], 1.0 / UNIT, OP.add, OP.mult, ky + [slot[t][1], "d0"], [("n", c)])
-
-    def where(c, t, rows):
-        y, ky = scan(rows)
+    def where(c, rows):
+        if c is None:
+            y, ky = scan(rows)
+        else:
+            for k, (row, keys) in enumerate(rows):
+                a = 1536 * c + 768 * k
+                lifted(T.d0[:, a:a + 768:3], row, keys + ["d0"], [("n", c, k)])
+            y, ky = T.d0[:, 1536 * c + 45:1536 * c + 1534:48], both("n", c)
         o, ko, oa = small(32, "smu")
-        ts(o, y, mlift, None, OP.add, None, ky + [kmlift], [ko])
-        if c is not None:
-            new(c, t, y, ky)
+        ts(o, y, lift, None, OP.subtract, None, ky + [klift], [ko])
         return oa, ko
 
     def ident(t):
@@ -551,78 +389,62 @@ def rank_program(g, core, T, topo):
         return [pick(T.Dd[:, 512 * t:512 * t + 512], ["D%d" % t], *l2) for l2 in (la16(l), lb16(l))]
 
     rk = [small(1) for _ in range(R)]
+    turn = [small(2, "smu") for _ in range(R)]
 
     def limit(t):
         kb, kkb, _ = small(32)
         kt, kkt, ka = small(32)
-        c8, kc8, _ = small(12)
+        c8, kc8, _ = small(8)
         own, kown, _ = small(1)
         ts(kb, fr8, s2[t][0][0], s2[t][1][0], OP.add, OP.add, [kfr8, s2[t][0][1], s2[t][1][1]], [kkb])
-        V(lambda e: e.transpose(kt, kb), 32, [kkb], [kkt])
+        V(lambda e: e.transpose(kt, kb), [kkb], [kkt])
         ts(own, gfr, s1[t][0][0], s1[t][1][0], OP.add, OP.add, [kgfr, s1[t][0][1], s1[t][1][1]], [kown])
-        op({"s": (lambda e: e.activation(c8, T.smf[:, ka:ka + 12], AF.Sign, bias=own, scale=-1.0, accum_out=rk[t][0]), (20.0, 64, 0, 0))},
+        op({"s": lambda e: e.activation(c8, T.smf[:, ka:ka + 8], AF.Sign, bias=own, scale=-1.0, accum_out=rk[t][0])},
            [kkt, kown], [kc8, rk[t][1]])
+        a = turn[t][2]
+        ts(T.smu[:, a:a + 1], rk[t][0], -4.0, base, OP.is_lt, OP.add, [rk[t][1], kbase], [turn[t][1]])
 
-    def limits(c, t):
-        out, col = T.d0[:, 96 * c + 2:96 * c + 96:3], rk[t][0]
-        op({"v": (lambda e: e.tensor_scalar(out, zero, col, None, OP.add), (0.0, 64, 0, 0)),
-            "s": (lambda e: e.activation(out, zero, AF.Identity, bias=col), (0.0, 64, 0, 0))}, [kzero, rk[t][1], "d0"], [("lim", c)])
-
-    def merge(c, t, off):
+    def merge(c, t, off, parts, outs, shift, w):
         oa, ko = off
-        win, wk = T.sgw[:, 272 * t:272 * t + 257], [("pad", t), ("sgw", t, 0), ("sgw", t, 1), khalf1, ko]
-        limits(c, t)
-        parts = 2 if c in SPLIT else 1
-        w = 256 // parts
+        win, wk = T.sgw[:, 272 * t:272 * t + 257], ["pad", ("sgw", t, 0), ("sgw", t, 1), mid[t][1]]
         for k in range(2):
-            i = used["gx"]
-            used["gx"] = i + 1
-            row = T.gx[:, 256 * i:256 * i + 256]
-            for d in range(parts):
-                o = oa + 16 * k + 8 * d
-                out, in_ = T.gx[:, 256 * i + w * d:256 * i + w * d + w], win.indirect(T.smu[:, o:o + 16 // parts])
-                op({"v": (lambda e, out=out, in_=in_: e.tensor_scalar(out, in_, 0.5, half1, OP.mult, OP.add), (50.0, 0, w, 0)),
-                    "s": (lambda e, out=out, in_=in_: e.activation(out, in_, AF.Identity, bias=half1, scale=0.5), (65.0, 0, w, 0))}, wk, [("gx", i, d)])
+            row, keys = pick(win, wk, oa + 16 * k, ko, parts, LIFT / 2.0, mid[t][0])
             a = 1536 * c + 768 * k
-            V(lambda e, a=a, row=row: e.tensor_tensor_scan(T.d1[:, a:a + 768:3], T.st[:, 256:512], row, 0.0, OP.add, OP.max),
-              128, [("gx", i, d) for d in range(parts)] + [("st", 256)], [("flag", c, k)])
+            lifted(T.d1[:, a:a + 768:3], row, keys, [("flag", c, k)])
         for k in range(2):
-            a, b = 1536 * c + 768 * k + 45, 96 * c + 48 * k
-            V(lambda e, a=a, b=b: e.tensor_tensor_scan(T.rs[:, b:b + 48], T.d0[:, b:b + 48], T.d1[:, a:a + 753:16], 0.0, OP.min, OP.max),
-              48, [("flag", c, k), ("old", c), ("bak", c, k), ("n", c), ("lim", c), "d0"], [("rs", c, k)])
-
-    def merge_rows(c, t, rows):
-        y, ky = scan(rows)
-        limits(c, t)
-        new(c, t, y, ky)
-        ts(flags(c), y, mlift, None, OP.add, None, ky + [kmlift], [("flag", c, 0), ("flag", c, 1)])
-        a, b = 1536 * c + 45, 96 * c
-        V(lambda e: e.tensor_tensor_scan(T.rs[:, b:b + 96], T.d0[:, b:b + 96], T.d1[:, a:a + 1521:16], 0.0, OP.min, OP.max),
-          96, [("flag", c, 0), ("flag", c, 1), ("old", c), ("bak", c, 0), ("bak", c, 1), ("n", c), ("lim", c), "d0"], kres(c))
+            a, b = 1536 * c + 768 * k, 96 * c + 48 * k
+            V(lambda e, a=a, b=b: e.tensor_tensor_scan(T.rs[:, b:b + 48], T.d0[:, a + 29:a + 782:16], T.d1[:, a + 45:a + 798:16], 0.0, OP.add, OP.max),
+              [("flag", c, k), ("old", c, k), ("bak", c), ("n", c, k), "d0"], [("rs", c, k)])
+            u = turn[t][2]
+            ts(outs[k], T.rs[:, b:b + 48].indirect(T.smu[:, u:u + 1]), shift, None, OP.add, None, [("rs", c, k), turn[t][1]], [w[k]])
 
     def settle(c, t, off):
-        merge(c, t, off)
-        for half in range(2):
-            a = zl[t + 1] + 16 * half
-            ts(T.smu[:, a:a + 16], result(c, half), UNIT, float(SL), OP.mult, OP.add, [("rs", c, half)], [("zl", t + 1, half, 0)])
+        a = zl[t + 1]
+        merge(c, t, off, 2, [T.smu[:, a:a + 16], T.smu[:, a + 16:a + 32]], -1.0, [("zl", t + 1, k, 0) for k in range(2)])
 
-    def before(c, b):
-        V(lambda e: e.tensor_copy(older(c), result(b)), 32, kres(b), [("old", c)])
+    def kept(rows, c, outs, w):
+        y, ky = scan(rows)
+        n, kn, _ = small(32)
+        ts(n, y, lift, 512.0, OP.subtract, OP.add, ky + [klift], [kn])
+        for out, k in zip(outs, w):
+            tt(out, n, backed(c), OP.max, [kn, ("bak", c)], k)
 
     inverse(0)
     operands(0)
-    w01 = where(0, 0, find(0, 1))
+    w01 = where(0, find(0, 1))
     for p in range(4):
         out, in_ = T.F[:, SL * p:SL * p + 512], T.X0[:, p:2048:4]
-        op({"g": (lambda e, out=out, in_=in_: e.affine_select(out, in_, [[0, 512]], OP.is_equal, 0.0, 0, 0), (170.0, 1024, 0, 0)),
-            "v": (lambda e, out=out, in_=in_: e.tensor_copy(out, in_), (0.0, 256, 0, 0))}, ["X0"], [("Fx", p)])
-    V(lambda e: e.quantize_mx(T.uq[:], T.uqs[:], T.uin[:]), 150, ["uin"], ["uq"])
-    op({"v": (lambda e: e.tensor_copy(T.up[:].bitcast(dt.uint32), T.uq[:].bitcast(dt.uint32).indirect(U16)), (50.0, 0, 256, 0))},
-       ["uq", (kU16, 0), (kU16, 1)], ["up"])
-    copy(T.ups[:], T.uqs[:].indirect(U16), 256, ["uq", (kU16, 0), (kU16, 1)], ["ups"], True)
+        op({"g": lambda e, out=out, in_=in_: e.affine_select(out, in_, [[0, 512]], OP.is_equal, 0.0, 0, 0),
+            "s": lambda e, out=out, in_=in_: e.activation(out, in_, AF.Copy),
+            "v": lambda e, out=out, in_=in_: e.tensor_copy(out, in_)}, ["X0"], [("Fx", p)])
+    V(lambda e: e.quantize_mx(T.uq[:], T.uqs[:], T.uin[:]), ["uin"], ["uq"])
+    V(lambda e: e.tensor_copy(T.up[:].bitcast(dt.uint32), T.uq[:].bitcast(dt.uint32).indirect(U16)), ["uq", (kU16, 0), (kU16, 1)], ["up"])
+    copy(T.ups[:], T.uqs[:].indirect(U16), ["uq", (kU16, 0), (kU16, 1)], ["ups"])
     for b in range(4):
-        V(lambda e, b=b: e.quantize_mx(T.eq[:, 128 * b:128 * b + 128], T.eqs[:, 128 * b:128 * b + 128], T.ez[:, 4 - b:516 - b]), 150, ["ez"], [("eq", b)])
+        V(lambda e, b=b: e.quantize_mx(T.eq[:, 128 * b:128 * b + 128], T.eqs[:, 128 * b:128 * b + 128], T.ez[:, 16 - b:528 - b]),
+          [("ez", 0), ("ez", 1)], [("eq", b)])
     layer(0, 0)
+    op({"y": lambda q: dmas(q, "lv", [(T.vin[:], T.v[:])], [("lz", 0, 1)], ["vin"])}, [("lz", 0, 1)], ["vin"], "load")
     scores(0, 0)
     layer(0, 1)
     scores(0, 1)
@@ -631,62 +453,69 @@ def rank_program(g, core, T, topo):
 
     operands(1)
     inverse(1)
-    w12, w0 = where(3, 1, find(1, 2)), where(None, 0, ident(0))
+    w12, w0 = where(1, find(1, 2)), where(None, ident(0))
     layer(1, 0)
     scores(1, 0)
-    tt(T.val[:, 1:257], T.sgw[:, 1:257], T.jr1[:], OP.mult, [("sgw", 0, 0), ("sgw", 0, 1), "jr1"], ["val"], 256)
-    regs = [pick(T.val[:, 0:257], ["val", ("pad", R)], T.smu[:, w0[0] + 16 * k:w0[0] + 16 * k + 16], w0[1]) for k in range(2)]
+    v0 = 272 * R
+    tt(T.sgw[:, v0 + 1:v0 + 257], T.sgw[:, 1:257], T.jr[:, 256:512], OP.min, [("sgw", 0, 0), ("sgw", 0, 1), "jrs"], ["val"])
+    drop, kdrop, _ = small(1)
+    ts(drop, rk[0][0], -4.0, -2048.0, OP.is_lt, OP.mult, [rk[0][1]], [kdrop])
+    regs = [pick(T.sgw[:, v0:v0 + 257], ["val", "pad", kdrop], w0[0] + 16 * k, w0[1], 1, 1024.0, drop) for k in range(2)]
     g0 = 256 * regs[0][1][0][1]
-    merge_rows(1, 0, [pick(T.gx[:, g0:g0 + 512], regs[0][1] + regs[1][1], *l) for l in (la16(2), lb16(2))])
-    before(3, 1)
+    kept([pick(T.gx[:, g0:g0 + 512], regs[0][1] + regs[1][1], *l) for l in (la16(2), lb16(2))], 1, [older(1)], [both("old", 1)])
     layer(1, 1)
     scores(1, 1)
     limit(1)
-    settle(3, 1, w12)
+    settle(1, 1, w12)
 
     operands(2)
     inverse(2)
-    w1, w2 = [where(c, t, ident(t)) for c, t in ((4, 1), (5, 2))]
-    merge_rows(2, 0, regs)
-    before(4, 2)
-    merge(4, 1, w1)
-    before(5, 4)
-    gm, kgm, _ = small(32)
-    affine(gm, result(2), -1.0, 0.0, kres(2), [kgm])
-    V(lambda e: e.quantize_mx(T.vq[:], T.vqs[:], T.vin[:]), 150, ["vin"], ["vq"])
+    w1, w2 = [where(c, ident(t)) for c, t in ((2, 1), (3, 2))]
+    kept(regs, 2, [older(2), backed(3)], [both("old", 2), [("bak", 3)]])
+    merge(2, 1, w1, 1, [older(3, 0), older(3, 1)], 0.0, both("old", 3))
+    V(lambda e: e.quantize_mx(T.vq[:], T.vqs[:], T.vin[:]), ["vin"], ["vq"])
     layer(2, 0)
     scores(2, 0)
     layer(2, 1)
     scores(2, 1)
     limit(2)
-    ts(backed(5), gm, rk[2][0], -1.0, OP.max, OP.mult, [kgm, rk[2][1]], [("bak", 5, 0), ("bak", 5, 1)])
-    settle(5, 2, w2)
+    settle(3, 2, w2)
 
     def store(q, sem, pairs, r, w):
-        op({q: (lambda q: dmas(q, sem, pairs, r, w), (60.0 * len(pairs), 0, 0, 0))}, r, w, "dma")
-        ops[-1]["busy"] = 320.0 if len(pairs) == 1 else 150.0
+        op({q: lambda q: dmas(q, sem, pairs, r, w)}, r, w, "dma")
 
+    lo = 0
+    for n in TCUT:
+        for p in range(4):
+            win, wk = window(3, p)
+            a = zl[3] + lo // 16
+            copy(T.Tt[:, 4 * lo + p:4 * (lo + n):4], win.indirect(T.smu[:, a:a + n // 16]),
+                 wk + [("zl", 3, k, 0) for k in sorted({lo // 256, (lo + n - 1) // 256})], [("T", c, p) for c in range(lo // 128, (lo + n) // 128)])
+        lo += n
     for c in range(4):
         lo, hi = 128 * c, 128 * c + 128
-        for p in range(4):
-            (win, wk), (off, ko) = window(3, p), zoff(3, c // 2, p, c % 2)
-            copy(T.Tt[:, 512 * c + p:512 * c + 512:4], win.indirect(off), 128, wk + [ko], [("T", c, p)], True)
-        V(lambda e, lo=lo, hi=hi: e.quantize_mx(T.oq[:, lo:hi], T.oqs[:, lo:hi], T.Tt[:, 4 * lo:4 * hi]), 150, [("T", c, p) for p in range(4)], [("oq", c)])
+        V(lambda e, lo=lo, hi=hi: e.quantize_mx(T.oq[:, lo:hi], T.oqs[:, lo:hi], T.Tt[:, 4 * lo:4 * hi]), [("T", c, p) for p in range(4)], [("oq", c)])
         mm(4 + c, T.vq[:], T.vqs[:], T.oq[:, lo:hi], T.oqs[:, lo:hi], ["vq", ("oq", c)])
-        copy(T.yo[:, lo:hi], bank(4 + c), 128, [("bk", 4 + c)], [("yo", c)], False)
-        store("y", "so%d" % c, [(T.oc[:, 4 * lo:4 * hi], T.oq[:, lo:hi].bitcast(dt.uint8))], [("oq", c)], [("oc", c)])
-        store("y", "sy%d" % c, [(T.y[:, lo:hi], T.yo[:, lo:hi])], [("yo", c)], [("y", c)])
+        copy(T.yo[:, lo:hi], bank(4 + c), [("bk", 4 + c)], [("yo", c)])
+    c = 0
+    for n in OCUT:
+        lo, hi = 128 * c, 128 * (c + n)
+        store("y", "so%d" % c, [(T.oc[:, 4 * lo:4 * hi], T.oq[:, lo:hi].bitcast(dt.uint8))], [("oq", k) for k in range(c, c + n)], [("oc", c)])
+        c += n
+    c = 0
+    for n in YCUT:
+        lo, hi = 128 * c, 128 * (c + n)
+        store("y", "sy%d" % c, [(T.y[:, lo:hi], T.yo[:, lo:hi])], [("yo", k) for k in range(c, c + n)], [("y", c)])
+        c += n
     store("s", "sos", [(T.osc[4 * k:4 * k + 4, :], T.oqs[32 * k:32 * k + 4, :]) for k in range(4)], [("oq", c) for c in range(4)], ["osc"])
     pl, kpl, _ = small(32)
     ot, kot, oa = small(32)
-    affine(pl, result(5), UNIT, float(SL), kres(5), [kpl])
-    V(lambda e: e.transpose(ot, pl), 32, [kpl], [kot])
+    V(lambda e: e.tensor_copy(pl, T.smu[:, zl[3]:zl[3] + 32]), [("zl", 3, 0, 0), ("zl", 3, 1, 0)], [kpl])
+    V(lambda e: e.transpose(ot, pl), [kpl], [kot])
     store("y", "som", [(T.om[k:8:2, :], T.smf[:, oa + 16 * k:oa + 16 * k + 16]) for k in range(2)], [kot], ["om"])
 
-    if "order" not in PLAN:
-        PLAN["order"] = make_plan(ops, ready)
-    for i, q in PLAN["order"]:
-        emit(ops[i], q)
+    for w in ORDER.split():
+        emit(ops[int(w[:-1])], w[-1])
     for s in SEMAPHORES:
         if known["g"].get(s, 0) < count.get(s, 0):
             g.wait_ge(T.sem[s], count[s])

from concourse.mybir import dt, AluOpType, ActivationFunctionType

OP = AluOpType
AF = ActivationFunctionType
R = 3
STEP = [1, 2, 4]
LIFT = 1536
DEEP = -8192
SL = 1280
HALF = "float16"
NS = 4
TCUT = (128, 256, 128)
OCUT = (1, 2, 1)
YCUT = (1, 2, 1)
ORDER = """
10v 2g 1g 32v 0g 33v 15v 14v 29v 21v 17v 12v 16v 22s 18v 23s 4g 26s 19v 7s 30g 35v 5v 11g 25s 3g 8g 38v 37v 41v 40s 9g 39v 20s 34v 42v 43s 13v 45v 24s 27s 36v 47v 6g 50v 48v 49v 52v 46v 53v 54v 72s 99g 44v 73s 51v 80v 71s 81v 74s 79v 75s 82v 77s 85v 76s 83v 78s 67v 84g 55s 86v 87v 61s 68v 88v 62s 69v 56s 89v 100v 90g 57v 70v 102s 97g 31v 92s 58v 194v 103v 91s 104v 59v 60v 101v 98g 94v 106v 109t 93v 107t 108t 113s 110t 111s 112s 130t 116y 114s 129t 96g 132t 134s 115v 131t 133s 185v 136s 117t 135s 118t 95v 121t 119s 123t 137v 120s 186v 122s 138t 124s 139t 105v 142t 140s 187v 148t 141s 125t 155s 146t 152v 144t 150v 127t 158v 156s 151v 159s 188v 153s 157v 149s 160v 147s 154v 126s 161v 219v 143s 163v 162v 128s 164v 145s 167v 165s 195v 166s 175v 168s 173v 169s 174v 170s 176v 171s 179v 177v 172s 180v 190s 178g 181v 182v 28s 189s 196v 183v 218v 184g 192v 64v 220s 191v 221v 199t 197t 198t 203s 200t 201v 193v 223v 204s 202s 222s 205v 228t 229t 230t 232s 231t 233v 207t 234s 284v 212t 235s 206t 210t 209s 236v 213s 211s 63v 225v 208s 237t 238t 216t 224v 294v 239s 243t 289v 240s 247t 65v 214t 254s 226v 241t 255v 245t 258s 249v 227v 251v 257s 250v 256v 288v 252s 246s 260v 259v 244s 253v 242s 262v 248s 261v 215s 263v 217s 265v 264s 290v 267s 273v 272v 266s 275v 268s 274v 269s 278v 270s 276v 271s 279v 277g 301s 280v 281v 299s 66v 282v 295v 285v 283g 300v 286v 302v 307v 287v 296v 308t 291v 311t 309t 310t 315s 312s 314s 313s 332t 316v 331t 329t 336v 330t 335s 297v 317t 334s 333v 321t 292v 318t 319s 323t 337v 322s 320s 305v 298v 303v 339t 324v 338t 304v 325t 341s 293v 348t 306v 340s 327t 344t 350v 326s 346t 356v 355s 342t 352v 358s 351v 359v 345s 357v 353s 343s 360v 349s 361v 354v 347s 363v 328s 362v 364v 366v 367s 368v 365s 396v 373s 370v 372s 377v 397v 369v 371s 389y 378t 398y 375v 379s 376s 380v 392y 383v 374s 381t 390y 384t 382s 386v 385s 391y 395s 387t 393y 388v 394y
"""

SCRATCH = {
    "Lst": ("sbuf", [128, 176], "int32"),
    "X0": ("sbuf", [128, 2048], "bfloat16"),
    "F": ("sbuf", [128, 4 * SL], "bfloat16"),
    "Ag": ("sbuf", [128, 3072], "bfloat16"),
    "Z": ("sbuf", [128, 3072], "bfloat16"),
    "Hb": ("sbuf", [128, 3072], "bfloat16"),
    "Tt": ("sbuf", [128, 2048], "bfloat16"),
    "uin": ("sbuf", [128, 512], "bfloat16"),
    "vin": ("sbuf", [128, 512], "bfloat16"),
    "ez": ("sbuf", [128, 528], "bfloat16"),
    "sw": ("sbuf", [128, 16], "bfloat16"),
    "st": ("sbuf", [128, 256], "bfloat16"),
    "idw": ("sbuf", [128, 512], "bfloat16"),
    "m0r": ("sbuf", [128, 512], "bfloat16"),
    "jr": ("sbuf", [128, 512], "bfloat16"),
    "Dd": ("sbuf", [128, 1536], "bfloat16"),
    "sgw": ("sbuf", [128, 4 * 272], "bfloat16"),
    "sg2": ("sbuf", [128, 3 * 256], "bfloat16"),
    "gx": ("sbuf", [128, 256 * 24], "bfloat16"),
    "gy": ("sbuf", [128, 256 * 12], HALF),
    "d0": ("sbuf", [128, 8 * 768 + 64], HALF),
    "d1": ("sbuf", [128, 8 * 768 + 64], HALF),
    "rs": ("sbuf", [128, 8 * 48], "float32"),
    "smi": ("sbuf", [128, 320], "int32"),
    "smf": ("sbuf", [128, 2560], "float32"),
    "smu": ("sbuf", [128, 1280], "uint16"),
    "yo": ("sbuf", [128, 512], "float32"),
    "ps": ("psum", [128, 4096], "float32"),
    "wq": ("sbuf", [128, 512], "float8_e4m3fn_x4"), "wqs": ("sbuf", [128, 512], "uint8"),
    "uq": ("sbuf", [128, 128], "float8_e4m3fn_x4"), "uqs": ("sbuf", [128, 128], "uint8"),
    "up": ("sbuf", [128, 256], "float8_e4m3fn_x4"), "ups": ("sbuf", [128, 256], "uint8"),
    "vq": ("sbuf", [128, 128], "float8_e4m3fn_x4"), "vqs": ("sbuf", [128, 128], "uint8"),
    "eq": ("sbuf", [128, 512], "float8_e4m3fn_x4"), "eqs": ("sbuf", [128, 512], "uint8"),
    "oq": ("sbuf", [128, 512], "float8_e4m3fn_x4"), "oqs": ("sbuf", [128, 512], "uint8"),
}
for _t in range(R):
    for _n in ("qz", "lz", "qh"):
        SCRATCH["%s%d" % (_n, _t)] = ("sbuf", [128, 256], "float8_e4m3fn_x4")
        SCRATCH["%ss%d" % (_n, _t)] = ("sbuf", [128, 256], "uint8")
ENG = {"v": "ve", "s": "ac", "t": "pe", "g": "gp"}
LOADS = ["lm", "la", "lb", "lx", "ll", "lu", "lw", "lv"]
STORES = ["so0", "so1", "so2", "so3", "sy0", "sy1", "sy2", "sy3", "som", "sos"]
SEMAPHORES = ["ve", "ac", "pe", "gp", "sent"] + ["arr%d%d" % (t, h) for t in range(R) for h in range(2)] + LOADS + STORES


def rank_program(g, core, T, topo):
    rank = T.rank_of(core)
    if rank is None:
        return
    queue = {"v": g.vector, "s": g.scalar, "t": g.tensor, "g": g, "y": g.sync}
    count = {}
    known = {q: {} for q in queue}
    writer, readers = {}, {}
    ops = []

    def need(q, ev):
        sem, val, snap = ev
        k = known[q]
        if k.get(sem, 0) < val:
            queue[q].wait_ge(T.sem[sem], val)
            k[sem] = val
        for s in snap:
            if k.get(s, 0) < snap[s]:
                k[s] = snap[s]

    def gate(q, r, w):
        own = ENG.get(q)
        evs = [writer[k] for k in r]
        for k in w:
            if k in writer and (writer[k][0] != own or q != "t"):
                evs.append(writer[k])
            evs += [e for e in readers.get(k, {}).values() if e[0] != own]
        for e in sorted(evs, key=lambda e: -e[1]):
            need(q, e)

    def note(ev, r, w):
        for k in w:
            writer[k] = ev
            readers[k] = {}
        for k in r:
            readers.setdefault(k, {})[ev[0]] = ev

    def dmas(q, sem, pairs, r=(), w=()):
        gate(q, r, w)
        for out, in_ in pairs:
            queue[q].dma_start(out, in_).then_inc(T.sem[sem], 16)
            count[sem] = count.get(sem, 0) + 16
        note((sem, count[sem], dict(known[q])), r, w)

    def emit(o, q):
        call = o["q"][q]
        if o["kind"] != "call":
            call(q)
            return
        gate(q, o["r"], o["w"])
        sem = ENG[q]
        call(queue[q]).then_inc(T.sem[sem], 1)
        count[sem] = count.get(sem, 0) + 1
        note((sem, count[sem], dict(known[q])), o["r"], o["w"])

    def op(qs, r, w, kind="call"):
        ops.append({"q": qs, "r": list(r), "w": list(w), "kind": kind})

    used = {"smf": 0, "smu": 0, "smi": 0, "gx": 0, "gy": 0}

    def small(n, buf="smf"):
        a = -(-used[buf] // (32 if n > 8 else 8)) * (32 if n > 8 else 8)
        used[buf] = a + n
        return T[buf][:, a:a + n], (buf, a), a

    def V(call, r=(), w=()):
        op({"v": call}, r, w)

    def G(call, r=(), w=()):
        op({"g": call}, r, w)

    def ts(out, in0, s1, s2, op0, op1, r, w):
        if op1 is None:
            V(lambda e: e.tensor_scalar(out, in0, s1, s2, op0), r, w)
        else:
            V(lambda e: e.tensor_scalar(out, in0, s1, s2, op0, op1), r, w)

    def tt(out, a, b, o, r, w):
        V(lambda e: e.tensor_tensor(out, a, b, o), r, w)

    def copy(out, in_, r, w):
        op({"v": lambda e: e.tensor_copy(out, in_), "s": lambda e: e.activation(out, in_, AF.Copy)}, r, w)

    def affine(out, in_, scale, bias, r, w):
        op({"v": lambda e: e.tensor_scalar(out, in_, scale, bias, OP.mult, OP.add),
            "s": lambda e: e.activation(out, in_, AF.Copy if isinstance(bias, float) else AF.Identity, bias=bias, scale=scale)}, r, w)

    def fill(out, v, n, key):
        op({"v": lambda e: e.memset(out, float(v)),
            "g": lambda e: e.iota(out, [[0, n]], v, 0, allow_small_or_imprecise_dtypes=True)}, [], [key])

    def pick(win, wkeys, off, okey, parts=1, scale=None, bias=None):
        i = used["gx"]
        used["gx"] = i + 1
        w, n = 256 // parts, 16 // parts
        for d in range(parts):
            out, in_ = T.gx[:, 256 * i + w * d:256 * i + w * d + w], win.indirect(T.smu[:, off + n * d:off + n * d + n])
            if scale is None:
                copy(out, in_, list(wkeys) + [okey], [("gx", i, d)])
            else:
                affine(out, in_, scale, bias, list(wkeys) + [okey], [("gx", i, d)])
        return T.gx[:, 256 * i:256 * i + 256], [("gx", i, d) for d in range(parts)]

    def lifted(out, row, keys, w):
        V(lambda e: e.tensor_tensor_scan(out, T.st[:], row, 0.0, OP.add, OP.max), list(keys) + ["st"], w)

    def scan(rows):
        first = used["gy"]
        for row, keys in rows:
            i = used["gy"]
            used["gy"] = i + 1
            lifted(T.gy[:, 256 * i:256 * i + 256], row, keys, [("gy", i)])
        return T.gy[:, 256 * first + 15:256 * first + 256 * len(rows):16], [("gy", first + k) for k in range(len(rows))]

    L = T.Lst
    dmas("y", "lm", [(L[:, 0:32], T.m[:])], w=["m_"])
    dmas("s", "lb", [(L[:, 80:128], T.lb[:])], w=["lb_"])
    dmas("y", "la", [(L[:, 32:80], T.la[:])], w=["la_"])
    dmas("y", "lx", [(T.X0[:], T.x[:])], w=["X0"])
    dmas("y", "ll", [(L[:, 128:176], T.ld[:])], w=["ld_"])
    dmas("y", "lu", [(T.uin[:], T.u[:])], w=["uin"])
    dmas("y", "lw", [(T.wq[:].bitcast(dt.uint8), T.wc[:]), (T.wqs[:], T.ws[:])], w=["wq"])

    vI, kvI, _ = small(16, "smi")
    pI, kpI, apI = small(32, "smi")
    kI, kkI, _ = small(8, "smi")
    c4, kc4, _ = small(1)
    G(lambda e: e.iota(T.idw[:, 0:256], [[1, 256]], -256, 0, allow_small_or_imprecise_dtypes=True), w=[("idw", 0)])
    G(lambda e: e.iota(vI, [[-1, 16]], 512, 1), w=[kvI])
    G(lambda e: e.iota(pI, [[0, 32]], 0, 1), w=[kpI])
    G(lambda e: e.iota(kI, [[16, 8]], 0, 0), w=[kkI])
    G(lambda e: e.iota(c4, [[0, 1]], -256, 4, allow_small_or_imprecise_dtypes=True), w=[kc4])
    affine(T.idw[:, 256:512], T.idw[:, 0:256], 1.0, 256.0, [("idw", 0)], [("idw", 1)])
    kidw = [("idw", 0), ("idw", 1)]
    op({"g": lambda e: e.iota(T.jr[:, 0:256], [[1, 256]], 1, 0, allow_small_or_imprecise_dtypes=True),
        "v": lambda e: e.tensor_scalar(T.jr[:, 0:256], T.idw[:, 0:256], 257.0, None, OP.add),
        "s": lambda e: e.activation(T.jr[:, 0:256], T.idw[:, 0:256], AF.Copy, bias=257.0)}, [("idw", 0)], ["jr1"])
    affine(T.jr[:, 256:512], T.idw[:, 0:256], 1.0 / 1024, 257.0 / 1024, [("idw", 0)], ["jrs"])
    eps, keps, _ = small(1)
    for t in range(R):
        fill(T.Dd[:, 512 * t:512 * t + 512], 0, 512, "D%d" % t)
    fill(T.sgw[:, 0:4 * 272:272], -1, 4, "pad")
    V(lambda e: e.memset(eps, 1e-37), w=[keps])
    ts(T.d0[:, 13:13 + 16 * 386:16], T.idw[:, 0:386], 0.0, float(DEEP), OP.mult, OP.add, kidw, ["d0"])
    vJ, kvJ, _ = small(16, "smi")
    p15, kp15, ap15 = small(16, "smi")
    p7, kp7, ap7 = small(32, "smi")
    pg, kpg, _ = small(1, "smi")
    s_a, ks_a, _ = small(16)
    s_b, ks_b, _ = small(16)
    r16, kr16, _ = small(16, "smu")
    ts(vJ, vI, 15, None, OP.bitwise_and, None, [kvI], [kvJ])
    ts(p15, T.smi[:, apI:apI + 16], 15, None, OP.bitwise_and, None, [kpI], [kp15])
    ts(s_a, vJ, 15, LIFT, OP.is_equal, OP.mult, [kvJ], [ks_a])
    ts(s_b, vJ, 0, DEEP, OP.is_equal, OP.mult, [kvJ], [ks_b])
    V(lambda e: e.tensor_copy(r16, p15), [kp15], [kr16])
    tt(T.sw[:], s_a, s_b, OP.add, [ks_a, ks_b], ["sw"])
    copy(T.st[:], T.sw[:].indirect(r16), ["sw", kr16], ["st"])
    lift, klift, _ = small(1)
    ts(lift, T.smi[:, ap15:ap15 + 1], 15, LIFT, OP.is_lt, OP.mult, [kp15], [klift])
    down = []
    for p in range(4):
        down.append(small(1))
        affine(down[p][0], lift, -4.0, float(1024 + p), [klift], [down[p][1]])
    mid = []
    for t in range(R):
        mid.append(small(1))
        affine(mid[t][0], lift, -2.0, float(512 + 256 * t - LIFT // 2), [klift], [mid[t][1]])
    base, kbase, _ = small(1)
    ts(base, T.smi[:, ap15:ap15 + 1], 3.0, 1.0, OP.mult, OP.add, [kp15], [kbase])
    fill(T.ez[:, 0:16], 0, 16, ("ez", 0))
    ts(T.ez[:, 16:528], T.idw[:], c4, None, OP.is_equal, None, kidw + [kc4], [("ez", 1)])
    fr8, kfr8, _ = small(32)
    gfr, kgfr, _ = small(1)
    U16, kU16, u0 = small(16, "smu")
    ts(p7, pI, 7, None, OP.bitwise_and, None, [kpI], [kp7])
    ts(pg, T.smi[:, apI:apI + 1], 4, None, OP.arith_shift_right, None, [kpI], [kpg])
    ts(fr8, p7, 0.125, None, OP.mult, None, [kp7], [kfr8])
    ts(gfr, pg, 0.125, None, OP.mult, None, [kpg], [kgfr])
    V(lambda e: e.tensor_copy(T.smu[:, u0:u0 + 8], kI), [kkI], [(kU16, 0)])
    ts(T.smu[:, u0 + 8:u0 + 16], T.smi[:, ap7:ap7 + 8], 16, None, OP.mult, None, [kp7], [(kU16, 1)])

    L16, kL16, l0 = small(128, "smu")
    D16, kD16, d0 = small(48, "smu")
    V(lambda e: e.tensor_copy(T.smu[:, l0:l0 + 32], L[:, 0:32]), ["m_"], [(kL16, 0)])
    V(lambda e: e.tensor_copy(T.smu[:, l0 + 32:l0 + 128], L[:, 32:128]), ["la_", "lb_"], [(kL16, 1)])

    def la16(t):
        return l0 + 32 + 16 * t, (kL16, 1)

    def lb16(t):
        return l0 + 80 + 16 * t, (kL16, 1)

    def inverse(t):
        n = 16 // NS
        for k in range(NS):
            a = d0 + 16 * t + n * k
            V(lambda e, a=a, k=k: e.tensor_copy(T.Dd[:, 512 * t:512 * t + 512].indirect(T.smu[:, a:a + n]), T.jr[:, 16 * n * k:16 * n * (k + 1)]),
              ["jr1", kD16], ["D%d" % t])

    for k in range(2):
        copy(T.m0r[:, 256 * k:256 * k + 256], T.idw[:].indirect(T.smu[:, l0 + 16 * k:l0 + 16 * k + 16]), kidw + [(kL16, 0)], [("m0r", k)])
    km0r = [("m0r", 0), ("m0r", 1)]
    rows0 = [pick(T.m0r[:], km0r, *la16(0)), pick(T.m0r[:], km0r, *lb16(0))]
    V(lambda e: e.tensor_copy(D16, L[:, 128:176]), ["ld_"], [kD16])
    zl0 = small(128, "smu")[2]
    zl = [None] + [small(32, "smu")[2] for _ in range(R)]
    for half in range(2):
        y, ky = scan([rows0[half]])
        for p in range(4):
            a = zl0 + 64 * half + 16 * p
            ts(T.smu[:, a:a + 16], y, 4.0, down[p][0], OP.mult, OP.add, ky + [down[p][1]], [("zl", 0, half, p)])

    def zoff(t, half, p, k):
        a = zl[t] + 16 * half + 8 * k if t else zl0 + 64 * half + 16 * p + 8 * k
        return T.smu[:, a:a + 8], ("zl", t, half, p if t == 0 else 0)

    def window(t, p):
        if t == 0:
            return T.X0[:], ["X0"]
        return T.F[:, SL * p:SL * p + 512 + 256 * t], [("Fx", p)] + [("Fn", s, h, p) for s in range(t) for h in range(2)]

    def send(t, h):
        qz, qs = T["qz%d" % t], T["qzs%d" % t]
        lo, hi = 128 * h, 128 * h + 128

        def call(q):
            dst = T.cores[rank ^ STEP[t]]
            rid, pid = topo.addr(dst)[:2]
            every, n = topo.mask(core, dst), 2 * len(topo.engines(core, dst))
            name = "arr%d%d" % (t, h)
            gate("g", [("qz", t, h)], [])
            g.remote_dma(T["lz%d" % t][:, lo:hi].bitcast(dt.uint8), qz[:, lo:hi].bitcast(dt.uint8), T.sem[name], T.sem.sent, pid, rid, every)
            g.remote_dma(T["lzs%d" % t][:, lo:hi], qs[:, lo:hi], T.sem[name], T.sem.sent, pid, rid, every)
            count["sent"] = count.get("sent", 0) + n
            count[name] = n
            writer[("lz", t, h)] = (name, n, {})
        op({"g": call}, [("qz", t, h)], [("lz", t, h)], "send")

    def operands(t):
        for h in range(2):
            for p in range(4):
                (win, wk), (off, ko) = window(t, p), zoff(t, 0, p, h)
                a = 1024 * t + 256 * p + 128 * h
                copy(T.Ag[:, a:a + 128], win.indirect(off), wk + [ko], [("A", t, h, p)])
        for h in range(2):
            lo, hi, z = 128 * h, 128 * h + 128, 1024 * t + 512 * h
            for p in range(4):
                (win, wk), (off, ko) = window(t, p), zoff(t, 1, p, h)
                a = 1024 * t + 256 * p + 128 * h
                tt(T.Z[:, z + p:z + 512:4], win.indirect(off), T.Ag[:, a:a + 128], OP.add, wk + [ko, ("A", t, h, p)], [("Z", t, h, p)])
            V(lambda e, lo=lo, hi=hi, z=z: e.quantize_mx(T["qz%d" % t][:, lo:hi], T["qzs%d" % t][:, lo:hi], T.Z[:, z:z + 512]),
              [("Z", t, h, p) for p in range(4)], [("qz", t, h)])
            send(t, h)

    def bank(k, n=128):
        return T.ps[:, 512 * k:512 * k + n]

    def mm(k, lq, ls, rq, rs, r):
        op({"t": lambda e: e.matmul_mx(bank(k), lq, ls, rq, rs, True, True)}, r, [("bk", k)])

    s1 = [[small(1) for _ in range(2)] for _ in range(R)]
    s2 = [[small(1) for _ in range(2)] for _ in range(R)]

    def layer(t, h):
        lo, hi, z = 128 * h, 128 * h + 128, 1024 * t + 512 * h
        for b in range(4):
            mm(4 * h + b, T.wq[:, 128 * b:128 * b + 128], T.wqs[:, 128 * b:128 * b + 128], T["lz%d" % t][:, lo:hi], T["lzs%d" % t][:, lo:hi], ["wq", ("lz", t, h)])
        for b in range(4):
            out = T.Hb[:, z + b:z + 512:4]
            op({"v": lambda e, b=b, out=out: e.tensor_scalar(out, bank(4 * h + b), 0.0, 0.015625, OP.max, OP.mult),
                "s": lambda e, b=b, out=out: e.activation(out, bank(4 * h + b), AF.Relu, scale=0.015625)}, [("bk", 4 * h + b)], [("H", t, h, b)])
        V(lambda e: e.quantize_mx(T["qh%d" % t][:, lo:hi], T["qhs%d" % t][:, lo:hi], T.Hb[:, z:z + 512]), [("H", t, h, b) for b in range(4)], [("qh", t, h)])

    def scores(t, h):
        lo, hi = 128 * h, 128 * h + 128
        q, s = T["qh%d" % t][:, lo:hi], T["qhs%d" % t][:, lo:hi]
        bs, bd = ((0, 1), (2, 3, 0, 1)) if h == 0 else ((4, 5), (6, 7, 2, 3))
        for k in range(2):
            mm(bs[k], T.up[:, 128 * k:128 * k + 128], T.ups[:, 128 * k:128 * k + 128], q, s, ["up", "ups", ("qh", t, h)])
        for k, name, out, sm in ((0, "sgw", T.sgw[:, 272 * t + 1 + lo:272 * t + 1 + hi], s1[t][h]), (1, "sg2", T.sg2[:, 256 * t + lo:256 * t + hi], s2[t][h])):
            op({"s": lambda e, k=k, out=out, sm=sm: e.activation(out, bank(bs[k]), AF.Sign, bias=eps, accum_out=sm[0])},
               [("bk", bs[k]), keps], [(name, t, h), sm[1]])
        for b in range(4):
            mm(bd[b], T.eq[:, 128 * b:128 * b + 128], T.eqs[:, 128 * b:128 * b + 128], q, s, [("eq", b), ("qh", t, h)])
            a = SL * b + 512 + 256 * t + lo
            copy(T.F[:, a:a + 128], bank(bd[b]), [("bk", bd[b])], [("Fn", t, h, b)])

    def older(c, k=None):
        a = 1536 * c + 61
        return T.d1[:, a:a + 1489:48] if k is None else T.d1[:, a + 768 * k:a + 768 * k + 721:48]

    def backed(c):
        return T.d1[:, 1536 * c + 77:1536 * c + 1566:48]

    def both(name, c):
        return [(name, c, 0), (name, c, 1)]

    def places(outs, y, ky, w):
        for out, k in zip(outs, w):
            ts(out, y, lift, 257.0, OP.subtract, OP.add, ky + [klift], k)

    y, ky = scan([pick(T.m0r[:], km0r, *l) for l in (la16(1), lb16(1))])
    places([older(0), backed(0)], y, ky, [both("old", 0), [("bak", 0)]])
    y, ky = scan([pick(T.m0r[:], km0r, *l) for l in (la16(2), lb16(2))])
    places([backed(1)], y, ky, [[("bak", 1)]])
    ts(backed(2), L[:, 0:32], 1.0, None, OP.add, None, ["m_"], [("bak", 2)])

    def where(c, rows):
        if c is None:
            y, ky = scan(rows)
        else:
            for k, (row, keys) in enumerate(rows):
                a = 1536 * c + 768 * k
                lifted(T.d0[:, a:a + 768:3], row, keys + ["d0"], [("n", c, k)])
            y, ky = T.d0[:, 1536 * c + 45:1536 * c + 1534:48], both("n", c)
        o, ko, oa = small(32, "smu")
        ts(o, y, lift, None, OP.subtract, None, ky + [klift], [ko])
        return oa, ko

    def ident(t):
        return [(T.Dd[:, 512 * t + 256 * k:512 * t + 256 * k + 256], ["D%d" % t]) for k in range(2)]

    def find(t, l):
        return [pick(T.Dd[:, 512 * t:512 * t + 512], ["D%d" % t], *l2) for l2 in (la16(l), lb16(l))]

    rk = [small(1) for _ in range(R)]
    turn = [small(2, "smu") for _ in range(R)]

    def limit(t):
        kb, kkb, _ = small(32)
        kt, kkt, ka = small(32)
        c8, kc8, _ = small(8)
        own, kown, _ = small(1)
        ts(kb, fr8, s2[t][0][0], s2[t][1][0], OP.add, OP.add, [kfr8, s2[t][0][1], s2[t][1][1]], [kkb])
        V(lambda e: e.transpose(kt, kb), [kkb], [kkt])
        ts(own, gfr, s1[t][0][0], s1[t][1][0], OP.add, OP.add, [kgfr, s1[t][0][1], s1[t][1][1]], [kown])
        op({"s": lambda e: e.activation(c8, T.smf[:, ka:ka + 8], AF.Sign, bias=own, scale=-1.0, accum_out=rk[t][0])},
           [kkt, kown], [kc8, rk[t][1]])
        a = turn[t][2]
        ts(T.smu[:, a:a + 1], rk[t][0], -4.0, base, OP.is_lt, OP.add, [rk[t][1], kbase], [turn[t][1]])

    def merge(c, t, off, parts, outs, shift, w):
        oa, ko = off
        win, wk = T.sgw[:, 272 * t:272 * t + 257], ["pad", ("sgw", t, 0), ("sgw", t, 1), mid[t][1]]
        for k in range(2):
            row, keys = pick(win, wk, oa + 16 * k, ko, parts, LIFT / 2.0, mid[t][0])
            a = 1536 * c + 768 * k
            lifted(T.d1[:, a:a + 768:3], row, keys, [("flag", c, k)])
        for k in range(2):
            a, b = 1536 * c + 768 * k, 96 * c + 48 * k
            V(lambda e, a=a, b=b: e.tensor_tensor_scan(T.rs[:, b:b + 48], T.d0[:, a + 29:a + 782:16], T.d1[:, a + 45:a + 798:16], 0.0, OP.add, OP.max),
              [("flag", c, k), ("old", c, k), ("bak", c), ("n", c, k), "d0"], [("rs", c, k)])
            u = turn[t][2]
            ts(outs[k], T.rs[:, b:b + 48].indirect(T.smu[:, u:u + 1]), shift, None, OP.add, None, [("rs", c, k), turn[t][1]], [w[k]])

    def settle(c, t, off):
        a = zl[t + 1]
        merge(c, t, off, 2, [T.smu[:, a:a + 16], T.smu[:, a + 16:a + 32]], -1.0, [("zl", t + 1, k, 0) for k in range(2)])

    def kept(rows, c, outs, w):
        y, ky = scan(rows)
        n, kn, _ = small(32)
        ts(n, y, lift, 512.0, OP.subtract, OP.add, ky + [klift], [kn])
        for out, k in zip(outs, w):
            tt(out, n, backed(c), OP.max, [kn, ("bak", c)], k)

    inverse(0)
    operands(0)
    w01 = where(0, find(0, 1))
    for p in range(4):
        out, in_ = T.F[:, SL * p:SL * p + 512], T.X0[:, p:2048:4]
        op({"g": lambda e, out=out, in_=in_: e.affine_select(out, in_, [[0, 512]], OP.is_equal, 0.0, 0, 0),
            "s": lambda e, out=out, in_=in_: e.activation(out, in_, AF.Copy),
            "v": lambda e, out=out, in_=in_: e.tensor_copy(out, in_)}, ["X0"], [("Fx", p)])
    V(lambda e: e.quantize_mx(T.uq[:], T.uqs[:], T.uin[:]), ["uin"], ["uq"])
    V(lambda e: e.tensor_copy(T.up[:].bitcast(dt.uint32), T.uq[:].bitcast(dt.uint32).indirect(U16)), ["uq", (kU16, 0), (kU16, 1)], ["up"])
    copy(T.ups[:], T.uqs[:].indirect(U16), ["uq", (kU16, 0), (kU16, 1)], ["ups"])
    for b in range(4):
        V(lambda e, b=b: e.quantize_mx(T.eq[:, 128 * b:128 * b + 128], T.eqs[:, 128 * b:128 * b + 128], T.ez[:, 16 - b:528 - b]),
          [("ez", 0), ("ez", 1)], [("eq", b)])
    layer(0, 0)
    op({"y": lambda q: dmas(q, "lv", [(T.vin[:], T.v[:])], [("lz", 0, 1)], ["vin"])}, [("lz", 0, 1)], ["vin"], "load")
    scores(0, 0)
    layer(0, 1)
    scores(0, 1)
    limit(0)
    settle(0, 0, w01)

    operands(1)
    inverse(1)
    w12, w0 = where(1, find(1, 2)), where(None, ident(0))
    layer(1, 0)
    scores(1, 0)
    v0 = 272 * R
    tt(T.sgw[:, v0 + 1:v0 + 257], T.sgw[:, 1:257], T.jr[:, 256:512], OP.min, [("sgw", 0, 0), ("sgw", 0, 1), "jrs"], ["val"])
    drop, kdrop, _ = small(1)
    ts(drop, rk[0][0], -4.0, -2048.0, OP.is_lt, OP.mult, [rk[0][1]], [kdrop])
    regs = [pick(T.sgw[:, v0:v0 + 257], ["val", "pad", kdrop], w0[0] + 16 * k, w0[1], 1, 1024.0, drop) for k in range(2)]
    g0 = 256 * regs[0][1][0][1]
    kept([pick(T.gx[:, g0:g0 + 512], regs[0][1] + regs[1][1], *l) for l in (la16(2), lb16(2))], 1, [older(1)], [both("old", 1)])
    layer(1, 1)
    scores(1, 1)
    limit(1)
    settle(1, 1, w12)

    operands(2)
    inverse(2)
    w1, w2 = [where(c, ident(t)) for c, t in ((2, 1), (3, 2))]
    kept(regs, 2, [older(2), backed(3)], [both("old", 2), [("bak", 3)]])
    merge(2, 1, w1, 1, [older(3, 0), older(3, 1)], 0.0, both("old", 3))
    V(lambda e: e.quantize_mx(T.vq[:], T.vqs[:], T.vin[:]), ["vin"], ["vq"])
    layer(2, 0)
    scores(2, 0)
    layer(2, 1)
    scores(2, 1)
    limit(2)
    settle(3, 2, w2)

    def store(q, sem, pairs, r, w):
        op({q: lambda q: dmas(q, sem, pairs, r, w)}, r, w, "dma")

    lo = 0
    for n in TCUT:
        for p in range(4):
            win, wk = window(3, p)
            a = zl[3] + lo // 16
            copy(T.Tt[:, 4 * lo + p:4 * (lo + n):4], win.indirect(T.smu[:, a:a + n // 16]),
                 wk + [("zl", 3, k, 0) for k in sorted({lo // 256, (lo + n - 1) // 256})], [("T", c, p) for c in range(lo // 128, (lo + n) // 128)])
        lo += n
    for c in range(4):
        lo, hi = 128 * c, 128 * c + 128
        V(lambda e, lo=lo, hi=hi: e.quantize_mx(T.oq[:, lo:hi], T.oqs[:, lo:hi], T.Tt[:, 4 * lo:4 * hi]), [("T", c, p) for p in range(4)], [("oq", c)])
        mm(4 + c, T.vq[:], T.vqs[:], T.oq[:, lo:hi], T.oqs[:, lo:hi], ["vq", ("oq", c)])
        copy(T.yo[:, lo:hi], bank(4 + c), [("bk", 4 + c)], [("yo", c)])
    c = 0
    for n in OCUT:
        lo, hi = 128 * c, 128 * (c + n)
        store("y", "so%d" % c, [(T.oc[:, 4 * lo:4 * hi], T.oq[:, lo:hi].bitcast(dt.uint8))], [("oq", k) for k in range(c, c + n)], [("oc", c)])
        c += n
    c = 0
    for n in YCUT:
        lo, hi = 128 * c, 128 * (c + n)
        store("y", "sy%d" % c, [(T.y[:, lo:hi], T.yo[:, lo:hi])], [("yo", k) for k in range(c, c + n)], [("y", c)])
        c += n
    store("s", "sos", [(T.osc[4 * k:4 * k + 4, :], T.oqs[32 * k:32 * k + 4, :]) for k in range(4)], [("oq", c) for c in range(4)], ["osc"])
    pl, kpl, _ = small(32)
    ot, kot, oa = small(32)
    V(lambda e: e.tensor_copy(pl, T.smu[:, zl[3]:zl[3] + 32]), [("zl", 3, 0, 0), ("zl", 3, 1, 0)], [kpl])
    V(lambda e: e.transpose(ot, pl), [kpl], [kot])
    store("y", "som", [(T.om[k:8:2, :], T.smf[:, oa + 16 * k:oa + 16 * k + 16]) for k in range(2)], [kot], ["om"])

    for w in ORDER.split():
        emit(ops[int(w[:-1])], w[-1])
    for s in SEMAPHORES:
        if known["g"].get(s, 0) < count.get(s, 0):
            g.wait_ge(T.sem[s], count[s])
